import numpy as np
import ml_dtypes


def mxq(x, axis, fmt="e4m3"):
    dtype, down = {"e4m3": (ml_dtypes.float8_e4m3fn, 7), "e5m2": (ml_dtypes.float8_e5m2, 14)}[fmt]
    v = np.moveaxis(np.asarray(x, np.float32).astype(ml_dtypes.bfloat16).astype(np.float64), axis, -1)
    blocks = v.reshape(v.shape[:-1] + (-1, 32))
    amax = np.abs(blocks).max(-1, keepdims=True)
    byte = np.maximum(np.where(amax > 0, np.frexp(amax)[1] - 1 + 127, 0) - down, 1)
    scale = np.exp2(byte - 127.0)
    codes = (blocks / scale).astype(np.float32).astype(dtype).astype(np.float64)
    return np.moveaxis((codes * scale).reshape(v.shape), -1, axis)


WIDE = False


def mx_kscale(k):
    if not WIDE:
        return np.ones(k)
    levels = np.array([10, -10, 5, -5, 0])
    if k % 512:
        return np.exp2(np.random.permutation(np.resize(levels, k // 32))).repeat(32)
    a = np.empty((k // 512, 16))
    for p in range(k // 512):
        a[p, :8] = np.random.permutation(np.resize(levels, 8))
        for g in range(8):
            far = levels[np.abs(levels - a[p, g]) >= 10]
            a[p, g + 8] = far[np.random.randint(len(far))]
    return np.exp2(a.ravel()).repeat(32)


def f64(x):
    return np.asarray(x).astype(np.float64)


def striped(idx):
    return np.tile(idx.reshape(-1, 16).T, (8, 1)).astype(np.uint16)


def unstriped(offs):
    return offs[:16].T.reshape(-1).astype(np.int64)


E2M1 = np.array([0.0, 0.5, 1.0, 1.5, 2.0, 3.0, 4.0, 6.0, -0.0, -0.5, -1.0, -1.5, -2.0, -3.0, -4.0, -6.0])


def pack_weight(w, fmt):
    k, n = w.shape
    w = f64(np.asarray(w, np.float32).astype(ml_dtypes.bfloat16)).reshape(k // 32, 32, n)
    amax = np.abs(w).max(1)
    if fmt == "e4m3":
        byte = np.frexp(amax)[1] - 1 + 127 - 7
    else:
        mant, ex = np.frexp(amax / 6.0)
        byte = np.where(mant > 0.5, ex, ex - 1) + 127
    byte = np.clip(np.where(amax > 0, byte, 1), 1, 254)
    scaled = (w * np.exp2(127.0 - byte)[:, None, :]).reshape(k, n).astype(np.float32)
    by_word = np.ascontiguousarray(scaled.reshape(k // 512, 128, 4, n).transpose(0, 1, 3, 2))
    if fmt == "e4m3":
        words = by_word.astype(ml_dtypes.float8_e4m3fn).view(np.uint8)
    else:
        c = by_word.astype(ml_dtypes.float4_e2m1fn).view(np.uint8) & 0xF
        words = (c[..., 0::2] | (c[..., 1::2] << 4)).reshape(k // 512, 128, 2 * n)
    return np.ascontiguousarray(words), np.ascontiguousarray(byte.astype(np.uint8).reshape(k // 512, 16, n))


def unpack_weight(words, scales, fmt):
    g, _, n = scales.shape
    words = np.ascontiguousarray(words).reshape(g, 128, n, -1)
    if fmt == "e4m3":
        vals = words.view(ml_dtypes.float8_e4m3fn).astype(np.float64)
    else:
        nib = np.empty((g, 128, n, 4), np.uint8)
        nib[..., 0::2] = words & 0xF
        nib[..., 1::2] = words >> 4
        vals = E2M1[nib]
    vals = vals * np.repeat(np.exp2(scales.astype(np.float64) - 127.0), 8, axis=1)[..., None]
    return vals.transpose(0, 1, 3, 2).reshape(g * 512, n)


def gelu(v):
    return 0.5 * v * (1.0 + np.tanh(np.sqrt(2.0 / np.pi) * (v + 0.044715 * v**3)))


def striped8(idx):
    return np.concatenate([v.reshape(-1, 16).T for v in idx]).astype(np.uint16)


def unstriped8(offs):
    return np.stack([offs[16 * g:16 * g + 16].T.reshape(-1) for g in range(8)]).astype(np.int64)


def runs(v, idx8):
    k = np.arange(v.shape[0])
    return v[k[:, None], idx8[k % 512 // 64]]


K, T, S, H, N = 1024, 2048, 1024, 1024, 384

def setup_inputs():
    n = np.random.standard_normal
    s = mx_kscale(K)[:, None]
    u = mx_kscale(H)[:, None]
    tab_words, tab_scales = pack_weight(n((K, T)) * s, "e4m3")
    offs = striped8(np.stack([np.random.permutation(T)[:S] for _ in range(8)]))
    ws = (n((K, H)) / np.sqrt(K) / s * u.T).astype(np.float32)
    wb_words, wb_scales = pack_weight(n((K, H)) / np.sqrt(K) / s, "e2m1")
    wn = (n((H, N)) / np.sqrt(H) / u).astype(np.float32)
    wd_words, wd_scales = pack_weight(n((H, N)) / np.sqrt(H) / u, "e4m3")
    kb = (0.5 * np.exp(0.3 * n(N))).astype(np.float32)
    return {"tab_words": tab_words, "tab_scales": tab_scales, "offs": offs,
            "ws": ws, "wb_words": wb_words, "wb_scales": wb_scales,
            "wn": wn, "wd_words": wd_words, "wd_scales": wd_scales, "kb": kb}

def reference(tab_words, tab_scales, offs, ws, wb_words, wb_scales,
              wn, wd_words, wd_scales, kb):
    v = runs(unpack_weight(tab_words, tab_scales, "e4m3"), unstriped8(offs))
    wb = unpack_weight(wb_words, wb_scales, "e2m1")
    wd = unpack_weight(wd_words, wd_scales, "e4m3")
    shear = mxq(f64(ws), 0, "e4m3").T @ v
    strat = wb.T @ v
    h = mxq(shear * strat, 0, "e4m3")
    num = mxq(f64(wn), 0, "e4m3").T @ h
    den = wd.T @ h
    return f64(kb)[:, None] + num / (1.0 + den * den)

@@ -1,0 +1,301 @@
+from contextlib import ExitStack
+
+import concourse.mybir as mybir
+
+K, T, S, H, N = 1024, 2048, 1024, 1024, 384
+FLOPS = 2 * (2 * K * H * S + 2 * H * N * S)
+
+F32 = mybir.dt.float32
+BF16 = mybir.dt.bfloat16
+I32 = mybir.dt.int32
+U32 = mybir.dt.uint32
+U16 = mybir.dt.uint16
+U8 = mybir.dt.uint8
+FP8X4 = mybir.dt.float8_e4m3fn_x4
+FP4X4 = mybir.dt.float4_e2m1fn_x4
+ACT = mybir.ActivationFunctionType
+MULT = mybir.AluOpType.mult
+ADD = mybir.AluOpType.add
+
+P = 128
+PACK = 4
+K_PASS = P * PACK
+PASSES = 2
+JB = 128
+BANK = 512
+N_TILES = N // P
+GATHER_CUTS = (0, 256, 512, 1024)
+OUT_CUTS = (0, 256, 512, 768, 896, 1024)
+
+
+def tile_list_mixing_closure_kernel(
+    tc, tab_words, tab_scales, offs, ws, wb_words, wb_scales, wn, wd_words, wd_scales, kb, out
+):
+    nc = tc.nc
+    with ExitStack() as ctx:
+        lists = ctx.enter_context(tc.tile_pool(name="lists", bufs=1))
+        keep = ctx.enter_context(tc.tile_pool(name="keep", bufs=1))
+        stage = ctx.enter_context(tc.tile_pool(name="stage", bufs=1))
+        work = ctx.enter_context(tc.tile_pool(name="work", bufs=2))
+        psum1 = ctx.enter_context(tc.psum_pool(name="psum1", bufs=4))
+        psum2 = ctx.enter_context(tc.psum_pool(name="psum2", bufs=2))
+
+        def staged(slot, shape, dtype, name):
+            return stage.tile(shape, dtype, name=name, tag=f"slot{slot}", align_bytes=64)
+
+        def held(shape, dtype, name):
+            return keep.tile(shape, dtype, name=name, align_bytes=64)
+
+        offsets = lists.tile([P, S // 16], U16, name="offsets")
+        nc.sync.dma_start(offsets[:], offs)
+
+        tab_scale_win = staged(0, [P, T], U8, "tab_scale_win")
+        nc.vector.memset(tab_scale_win[:].bitcast(I32), 0)
+        wb_scale_raw = held([P, PASSES, H], U8, "wb_scale_raw")
+        nc.vector.memset(wb_scale_raw[:].bitcast(I32), 0)
+
+        warm = held([P, 1], F32, "warm")
+        nc.vector.memset(warm[:], 1.0)
+        nc.scalar.activation(warm[:], warm[:], ACT.Abs_reciprocal_sqrt)
+
+        wb_raw = staged(1, [P, PASSES, 2 * H], U8, "wb_raw")
+        nc.sync.dma_start(wb_raw[:].bitcast(I32), wb_words.rearrange("a p c -> p a c").bitcast(I32))
+        for a in range(PASSES):
+            nc.sync.dma_start(tab_scale_win[a:P:8, :].bitcast(I32), tab_scales[a].bitcast(I32))
+        v_scales = [held([P, S], U8, f"v_scales{a}") for a in range(PASSES)]
+        wd_plane = held([P, PASSES, N], U8, "wd_plane")
+        for d in range(4):
+            nc.sync.dma_start(
+                wb_scale_raw[32 * d : 32 * d + 4].bitcast(I32),
+                wb_scales[:, 4 * d : 4 * d + 4, :].rearrange("a c n -> c a n").bitcast(I32),
+            )
+        tab_win = []
+        for a in range(PASSES):
+            win = staged(2 + a, [P, T], U32, f"tab_win{a}")
+            nc.sync.dma_start(
+                win[:].bitcast(I32), tab_words[a].rearrange("p t i -> p (t i)").bitcast(I32)
+            )
+            tab_win.append(win)
+
+        nc.vector.memset(v_scales[1][:].bitcast(I32), 0)
+        nc.vector.memset(wd_plane[:].bitcast(I32), 0)
+        for d in range(4):
+            nc.gpsimd.dma_start(
+                wd_plane[32 * d : 32 * d + 4].bitcast(I32),
+                wd_scales[:, 4 * d : 4 * d + 4, :].rearrange("a c n -> c a n").bitcast(I32),
+            )
+
+        picked_scales = staged(4, [P, S], U8, "picked_scales")
+        nc.vector.tensor_copy(picked_scales[:], tab_scale_win[:].indirect(offsets[:]))
+        nc.vector.tensor_copy(v_scales[0][:].bitcast(I32), picked_scales[:].bitcast(I32))
+        for a in range(PASSES):
+            for c in range(4):
+                if (a, c) != (0, 0):
+                    nc.scalar.dma_start(
+                        v_scales[a][c:P:32, :].bitcast(I32),
+                        picked_scales[8 * c + a : P : 32, :].bitcast(I32),
+                    )
+
+        ws_raw = {}
+
+        def load_ws(slot, a, b):
+            raw = staged(slot, [P, PACK, K_PASS], F32, f"ws_raw{a}{b}")
+            rows = ws[a * K_PASS : (a + 1) * K_PASS, b * K_PASS : (b + 1) * K_PASS]
+            nc.sync.dma_start(raw[:], rows.rearrange("(p i) r -> p i r", i=PACK))
+            ws_raw[a, b] = raw
+
+        load_ws(0, 0, 0)
+
+        wb_codes = [held([P, PASSES, 2 * K_PASS], U8, f"wb_codes{b}") for b in range(PASSES)]
+        wb_plane = [held([P, PASSES, K_PASS], U8, f"wb_plane{b}") for b in range(PASSES)]
+
+        def reorder_wb(b):
+            cols = slice(b * K_PASS, (b + 1) * K_PASS)
+            nc.vector.tensor_copy(
+                wb_codes[b][:].bitcast(U16).rearrange("p a (t g m) -> p a g t m", t=PACK, m=8),
+                wb_raw[:].bitcast(U16)[:, :, cols].rearrange("p a (g m t) -> p a g t m", t=PACK, m=8),
+            )
+            nc.vector.tensor_copy(
+                wb_plane[b][:].rearrange("p a (t g m) -> p a g t m", t=PACK, m=16),
+                wb_scale_raw[:, :, cols].rearrange("p a (g m t) -> p a g t m", t=PACK, m=16),
+            )
+
+        v_codes = [held([P, S], U32, f"v_codes{a}") for a in range(PASSES)]
+
+        def gather_words(a, piece):
+            lo, hi = GATHER_CUTS[piece], GATHER_CUTS[piece + 1]
+            nc.vector.tensor_copy(
+                v_codes[a][:, lo:hi], tab_win[a][:].indirect(offsets[:, lo // 16 : hi // 16])
+            )
+
+        def first_stage_pass(bank, codes, plane, a, jb, code_dtype, code_cols):
+            js = slice(jb * JB, (jb + 1) * JB)
+            for t in range(PACK):
+                nc.tensor.matmul_mx(
+                    out=bank[:, t, :],
+                    lhsT=codes[:, t * code_cols : (t + 1) * code_cols].bitcast(code_dtype),
+                    lhsT_scale=plane[:, t * P : (t + 1) * P],
+                    rhs=v_codes[a][:, js].bitcast(FP8X4),
+                    rhs_scale=v_scales[a][:, js],
+                    start=(a == 0 and t == 0),
+                    stop=(a == PASSES - 1 and t == PACK - 1),
+                )
+
+        strat = {}
+
+        def strat_banks(pairs):
+            banks = [psum1.tile([P, PACK, JB], F32, name="bank1") for pair in pairs]
+            for a in range(PASSES):
+                for bank, (b, jb) in zip(banks, pairs):
+                    first_stage_pass(bank, wb_codes[b][:, a, :], wb_plane[b][:, a, :], a, jb, FP4X4, 2 * P)
+            for bank, (b, jb) in zip(banks, pairs):
+                strat[b, jb] = held([P, JB, PACK], F32, f"strat{b}_{jb}")
+                nc.scalar.copy(strat[b, jb][:], bank[:].rearrange("p t j -> p j t"))
+
+        reorder_wb(0)
+        gather_words(0, 0)
+        reorder_wb(1)
+        load_ws(1, 1, 0)
+        load_ws(4, 0, 1)
+        gather_words(1, 0)
+        strat_banks([(0, 0), (0, 1), (1, 0), (1, 1)])
+        for piece in (1, 2):
+            for a in range(PASSES):
+                gather_words(a, piece)
+        load_ws(2, 1, 1)
+        for jb in range(2, S // JB):
+            for b in range(PASSES):
+                strat_banks([(b, jb)])
+
+        ws_codes, ws_plane = {}, {}
+        for b in range(PASSES):
+            for a in range(PASSES):
+                grouped = work.tile([P, PACK, P, PACK], BF16, name="ws_grouped", align_bytes=64)
+                nc.vector.tensor_copy(
+                    grouped[:].rearrange("p t m i -> p m t i"),
+                    ws_raw[a, b][:].rearrange("p i (m t) -> p m t i", t=PACK),
+                )
+                ws_codes[a, b] = held([P, K_PASS], U32, f"ws_codes{a}{b}")
+                ws_plane[a, b] = held([P, K_PASS], U8, f"ws_plane{a}{b}")
+                nc.vector.quantize_mx(
+                    out=ws_codes[a, b][:].bitcast(FP8X4),
+                    scales=ws_plane[a, b][:],
+                    in_=grouped[:].rearrange("p t m i -> p (t m i)"),
+                )
+
+        wn_grouped = held([P, PASSES * N * PACK], BF16, "wn_grouped")
+        for b in range(PASSES):
+            raw = staged((3, 0)[b], [P, PACK, N], F32, f"wn_raw{b}")
+            rows = wn[b * K_PASS : (b + 1) * K_PASS, :]
+            nc.sync.dma_start(raw[:], rows.rearrange("(p i) n -> p i n", i=PACK))
+            nc.scalar.copy(
+                wn_grouped[:, b * N * PACK : (b + 1) * N * PACK].rearrange(
+                    "p (g n i) -> p g i n", n=4, i=PACK
+                ),
+                raw[:].rearrange("p i (g n) -> p g i n", n=4),
+            )
+        wd_codes = staged(1, [P, PASSES, N], U32, "wd_codes")
+        nc.sync.dma_start(
+            wd_codes[:].bitcast(I32), wd_words.rearrange("a p n i -> p a (n i)").bitcast(I32)
+        )
+        kb_cols = staged(4, [P, N_TILES], F32, "kb_cols")
+        with nc.allow_non_contiguous_dma(reason="one value of kb for each partition"):
+            nc.sync.dma_start(kb_cols[:], kb.rearrange("(c p) -> p c", p=P))
+        wn_codes = held([P, PASSES * N], U32, "wn_codes")
+        wn_plane = held([P, PASSES * N], U8, "wn_plane")
+
+        def quantize_wn():
+            for lo, hi in ((0, 512), (512, 768)):
+                nc.vector.quantize_mx(
+                    out=wn_codes[:, lo:hi].bitcast(FP8X4),
+                    scales=wn_plane[:, lo:hi],
+                    in_=wn_grouped[:, PACK * lo : PACK * hi],
+                )
+
+        def make_h(piece, b):
+            lo, hi = OUT_CUTS[piece], OUT_CUTS[piece + 1]
+            h = work.tile([P, hi - lo, PACK], BF16, name=f"h{b}", align_bytes=64)
+            for jb in range(lo // JB, hi // JB):
+                bank = psum1.tile([P, PACK, JB], F32, name="bank1")
+                for a in range(PASSES):
+                    first_stage_pass(bank, ws_codes[a, b], ws_plane[a, b], a, jb, FP8X4, P)
+                nc.vector.tensor_tensor(
+                    h[:, jb * JB - lo : (jb + 1) * JB - lo, :],
+                    bank[:].rearrange("p t j -> p j t"),
+                    strat[b, jb][:],
+                    MULT,
+                )
+            return h
+
+        def quantize_h(h, b):
+            width = h.shape[1]
+            codes = work.tile([P, width], U32, name=f"h_codes{b}", align_bytes=64)
+            plane = work.tile([P, width], U8, name=f"h_plane{b}", align_bytes=64)
+            nc.vector.quantize_mx(
+                out=codes[:].bitcast(FP8X4), scales=plane[:], in_=h[:].rearrange("p j t -> p (j t)")
+            )
+            return codes, plane
+
+        def second_stage(packed, codes, plane, name):
+            width = packed[0][0].shape[1]
+            per_bank = min(N_TILES, BANK // width)
+            banks = []
+            for first in range(0, N_TILES, per_bank):
+                rows = range(first, min(first + per_bank, N_TILES))
+                bank = psum2.tile([P, len(rows), width], F32, name=name)
+                for c in rows:
+                    for b in range(PASSES):
+                        cols = slice(b * N + c * P, b * N + (c + 1) * P)
+                        nc.tensor.matmul_mx(
+                            out=bank[:, c - first, :],
+                            lhsT=codes[:, cols].bitcast(FP8X4),
+                            lhsT_scale=plane[:, cols],
+                            rhs=packed[b][0][:].bitcast(FP8X4),
+                            rhs_scale=packed[b][1][:],
+                            start=(b == 0),
+                            stop=(b == PASSES - 1),
+                        )
+                banks.append((slice(rows.start, rows.stop), bank))
+            return banks
+
+        def reciprocal_of_denominator(den, width):
+            shape = [P, N_TILES, width]
+            den_sq = work.tile(shape, F32, name="den_sq")
+            root = work.tile(shape, F32, name="root")
+            recip = work.tile(shape, F32, name="recip")
+            for rows, bank in den:
+                nc.scalar.activation(den_sq[:, rows, :], bank[:], ACT.Square)
+            nc.scalar.activation(root[:], den_sq[:], ACT.Abs_reciprocal_sqrt, bias=1.0)
+            nc.scalar.activation(recip[:], root[:], ACT.Square)
+            return recip
+
+        def finish(piece, num, recip):
+            lo, hi = OUT_CUTS[piece], OUT_CUTS[piece + 1]
+            shape = [P, N_TILES, hi - lo]
+            ratio = work.tile(shape, F32, name="ratio")
+            result = work.tile(shape, F32, name="result")
+            for rows, bank in num:
+                nc.vector.tensor_tensor(ratio[:, rows, :], bank[:], recip[:, rows, :], MULT)
+            for c in range(N_TILES):
+                nc.scalar.activation(
+                    result[:, c, :], ratio[:, c, :], ACT.Identity, bias=kb_cols[:, c : c + 1]
+                )
+            nc.sync.dma_start(out.rearrange("(c p) j -> p c j", p=P)[:, :, lo:hi], result[:])
+
+        pieces = len(OUT_CUTS) - 1
+        wd_flat = wd_codes[:].rearrange("p b n -> p (b n)")
+        wd_plane_flat = wd_plane[:].rearrange("p b n -> p (b n)")
+        packed = [quantize_h(make_h(0, b), b) for b in range(PASSES)]
+        quantize_wn()
+        for piece in range(pieces):
+            width = OUT_CUTS[piece + 1] - OUT_CUTS[piece]
+            more = piece + 1 < pieces
+            if more:
+                h_low = make_h(piece + 1, 0)
+            den = second_stage(packed, wd_flat, wd_plane_flat, "den")
+            recip = reciprocal_of_denominator(den, width)
+            num = second_stage(packed, wn_codes, wn_plane, "num")
+            if more:
+                h_high = make_h(piece + 1, 1)
+                packed = [quantize_h(h_low, 0), quantize_h(h_high, 1)]
+            finish(piece, num, recip)

@@ -23,6 +23,7 @@ K_PASS = P * PACK
 PASSES = 2
 JB = 128
 BANK = 512
+SLOT = 8192
 N_TILES = N // P
 GATHER_CUTS = (0, 256, 512, 1024)
 OUT_CUTS = (0, 256, 512, 768, 896, 1024)
@@ -40,8 +41,8 @@ def tile_list_mixing_closure_kernel(
         psum1 = ctx.enter_context(tc.psum_pool(name="psum1", bufs=4))
         psum2 = ctx.enter_context(tc.psum_pool(name="psum2", bufs=2))
 
-        def staged(slot, shape, dtype, name):
-            return stage.tile(shape, dtype, name=name, tag=f"slot{slot}", align_bytes=64)
+        def staged(offset, shape, dtype, name):
+            return stage.tile(shape, dtype, name=name, offset=offset, align_bytes=64)
 
         def held(shape, dtype, name):
             return keep.tile(shape, dtype, name=name, align_bytes=64)
@@ -49,62 +50,58 @@ def tile_list_mixing_closure_kernel(
         offsets = lists.tile([P, S // 16], U16, name="offsets")
         nc.sync.dma_start(offsets[:], offs)
 
-        tab_scale_win = staged(0, [P, T], U8, "tab_scale_win")
-        nc.vector.memset(tab_scale_win[:].bitcast(I32), 0)
-        wb_scale_raw = held([P, PASSES, H], U8, "wb_scale_raw")
+        tab_scale_win = held([P, T], U8, "tab_scale_win")
+        nc.gpsimd.memset(tab_scale_win[:].bitcast(I32), 0)
+        wb_scale_raw = staged(7 * SLOT, [P, PASSES, H], U8, "wb_scale_raw")
         nc.vector.memset(wb_scale_raw[:].bitcast(I32), 0)
 
         warm = held([P, 1], F32, "warm")
         nc.vector.memset(warm[:], 1.0)
         nc.scalar.activation(warm[:], warm[:], ACT.Abs_reciprocal_sqrt)
 
-        wb_raw = staged(1, [P, PASSES, 2 * H], U8, "wb_raw")
+        wb_raw = held([P, PASSES, 2 * H], U8, "wb_raw")
         nc.sync.dma_start(wb_raw[:].bitcast(I32), wb_words.rearrange("a p c -> p a c").bitcast(I32))
         for a in range(PASSES):
             nc.sync.dma_start(tab_scale_win[a:P:8, :].bitcast(I32), tab_scales[a].bitcast(I32))
         v_scales = [held([P, S], U8, f"v_scales{a}") for a in range(PASSES)]
-        wd_plane = held([P, PASSES, N], U8, "wd_plane")
         for d in range(4):
             nc.sync.dma_start(
                 wb_scale_raw[32 * d : 32 * d + 4].bitcast(I32),
                 wb_scales[:, 4 * d : 4 * d + 4, :].rearrange("a c n -> c a n").bitcast(I32),
             )
+        ws_raw = {}
+
+        def load_ws(a, b):
+            raw = staged((2 * b + a) * SLOT, [P, PACK, K_PASS], F32, f"ws_raw{a}{b}")
+            rows = ws[a * K_PASS : (a + 1) * K_PASS, b * K_PASS : (b + 1) * K_PASS]
+            nc.sync.dma_start(raw[:], rows.rearrange("(p i) r -> p i r", i=PACK))
+            ws_raw[a, b] = raw
+
         tab_win = []
         for a in range(PASSES):
-            win = staged(2 + a, [P, T], U32, f"tab_win{a}")
+            win = staged((4 + a) * SLOT, [P, T], U32, f"tab_win{a}")
             nc.sync.dma_start(
                 win[:].bitcast(I32), tab_words[a].rearrange("p t i -> p (t i)").bitcast(I32)
             )
             tab_win.append(win)
+            load_ws(a, 0)
 
         nc.vector.memset(v_scales[1][:].bitcast(I32), 0)
-        nc.vector.memset(wd_plane[:].bitcast(I32), 0)
-        for d in range(4):
-            nc.gpsimd.dma_start(
-                wd_plane[32 * d : 32 * d + 4].bitcast(I32),
-                wd_scales[:, 4 * d : 4 * d + 4, :].rearrange("a c n -> c a n").bitcast(I32),
-            )
 
-        picked_scales = staged(4, [P, S], U8, "picked_scales")
+        picked_scales = staged(3 * SLOT - S // 2, [P, S], U8, "picked_scales")
         nc.vector.tensor_copy(picked_scales[:], tab_scale_win[:].indirect(offsets[:]))
         nc.vector.tensor_copy(v_scales[0][:].bitcast(I32), picked_scales[:].bitcast(I32))
         for a in range(PASSES):
             for c in range(4):
                 if (a, c) != (0, 0):
-                    nc.scalar.dma_start(
+                    queue = nc.gpsimd if (a, c) == (1, 3) else nc.scalar
+                    queue.dma_start(
                         v_scales[a][c:P:32, :].bitcast(I32),
                         picked_scales[8 * c + a : P : 32, :].bitcast(I32),
                     )
 
-        ws_raw = {}
-
-        def load_ws(slot, a, b):
-            raw = staged(slot, [P, PACK, K_PASS], F32, f"ws_raw{a}{b}")
-            rows = ws[a * K_PASS : (a + 1) * K_PASS, b * K_PASS : (b + 1) * K_PASS]
-            nc.sync.dma_start(raw[:], rows.rearrange("(p i) r -> p i r", i=PACK))
-            ws_raw[a, b] = raw
-
-        load_ws(0, 0, 0)
+        for a in range(PASSES):
+            load_ws(a, 1)
 
         wb_codes = [held([P, PASSES, 2 * K_PASS], U8, f"wb_codes{b}") for b in range(PASSES)]
         wb_plane = [held([P, PASSES, K_PASS], U8, f"wb_plane{b}") for b in range(PASSES)]
@@ -143,8 +140,9 @@ def tile_list_mixing_closure_kernel(
 
         strat = {}
 
-        def strat_banks(pairs):
-            banks = [psum1.tile([P, PACK, JB], F32, name="bank1") for pair in pairs]
+        def strat_banks(pairs, spare=()):
+            banks = [psum1.tile([P, PACK, JB], F32, name="bank1") for pair in pairs[len(spare) :]]
+            banks.extend(psum2.tile([P, PACK, JB], F32, name=name) for name in spare)
             for a in range(PASSES):
                 for bank, (b, jb) in zip(banks, pairs):
                     first_stage_pass(bank, wb_codes[b][:, a, :], wb_plane[b][:, a, :], a, jb, FP4X4, 2 * P)
@@ -155,50 +153,73 @@ def tile_list_mixing_closure_kernel(
         reorder_wb(0)
         gather_words(0, 0)
         reorder_wb(1)
-        load_ws(1, 1, 0)
-        load_ws(4, 0, 1)
+        wd_plane = staged(7 * SLOT, [P, PASSES, N], U8, "wd_plane")
+        nc.vector.memset(wd_plane[:].bitcast(I32), 0)
+        for d in range(4):
+            nc.gpsimd.dma_start(
+                wd_plane[32 * d : 32 * d + 4].bitcast(I32),
+                wd_scales[:, 4 * d : 4 * d + 4, :].rearrange("a c n -> c a n").bitcast(I32),
+            )
+        gather_words(0, 1)
         gather_words(1, 0)
-        strat_banks([(0, 0), (0, 1), (1, 0), (1, 1)])
-        for piece in (1, 2):
-            for a in range(PASSES):
-                gather_words(a, piece)
-        load_ws(2, 1, 1)
-        for jb in range(2, S // JB):
+        gather_words(1, 1)
+        strat_banks(
+            [(0, 0), (0, 1), (1, 0), (1, 1), (0, 2), (1, 2), (0, 3), (1, 3)],
+            spare=("den", "den", "num", "num"),
+        )
+        for a in range(PASSES):
+            gather_words(a, 2)
+
+        ws_codes, ws_plane = {}, {}
+
+        def group_ws(a, b, copy):
+            grouped = held([P, PACK, P, PACK], BF16, f"ws_grouped{a}{b}")
+            copy(
+                grouped[:].rearrange("p t m i -> p m t i"),
+                ws_raw[a, b][:].rearrange("p i (m t) -> p m t i", t=PACK),
+            )
+            return grouped
+
+        def quantize_ws(a, b, grouped):
+            ws_codes[a, b] = held([P, K_PASS], U32, f"ws_codes{a}{b}")
+            ws_plane[a, b] = held([P, K_PASS], U8, f"ws_plane{a}{b}")
+            nc.vector.quantize_mx(
+                out=ws_codes[a, b][:].bitcast(FP8X4),
+                scales=ws_plane[a, b][:],
+                in_=grouped[:].rearrange("p t m i -> p (t m i)"),
+            )
+
+        low = [group_ws(0, 0, nc.scalar.copy), group_ws(1, 0, nc.vector.tensor_copy)]
+        for a in range(PASSES):
+            quantize_ws(a, 0, low[a])
+        high = [group_ws(a, 1, nc.vector.tensor_copy) for a in range(PASSES)]
+        for a in range(PASSES):
+            quantize_ws(a, 1, high[a])
+        for jb in (4, 5):
             for b in range(PASSES):
                 strat_banks([(b, jb)])
 
-        ws_codes, ws_plane = {}, {}
-        for b in range(PASSES):
-            for a in range(PASSES):
-                grouped = work.tile([P, PACK, P, PACK], BF16, name="ws_grouped", align_bytes=64)
-                nc.vector.tensor_copy(
-                    grouped[:].rearrange("p t m i -> p m t i"),
-                    ws_raw[a, b][:].rearrange("p i (m t) -> p m t i", t=PACK),
-                )
-                ws_codes[a, b] = held([P, K_PASS], U32, f"ws_codes{a}{b}")
-                ws_plane[a, b] = held([P, K_PASS], U8, f"ws_plane{a}{b}")
-                nc.vector.quantize_mx(
-                    out=ws_codes[a, b][:].bitcast(FP8X4),
-                    scales=ws_plane[a, b][:],
-                    in_=grouped[:].rearrange("p t m i -> p (t m i)"),
-                )
-
         wn_grouped = held([P, PASSES * N * PACK], BF16, "wn_grouped")
+        wn_raw = []
         for b in range(PASSES):
-            raw = staged((3, 0)[b], [P, PACK, N], F32, f"wn_raw{b}")
+            raw = staged((4 + b) * SLOT, [P, PACK, N], F32, f"wn_raw{b}")
             rows = wn[b * K_PASS : (b + 1) * K_PASS, :]
             nc.sync.dma_start(raw[:], rows.rearrange("(p i) n -> p i n", i=PACK))
+            wn_raw.append(raw)
+
+        def group_wn(b):
             nc.scalar.copy(
                 wn_grouped[:, b * N * PACK : (b + 1) * N * PACK].rearrange(
                     "p (g n i) -> p g i n", n=4, i=PACK
                 ),
-                raw[:].rearrange("p i (g n) -> p g i n", n=4),
+                wn_raw[b][:].rearrange("p i (g n) -> p g i n", n=4),
             )
-        wd_codes = staged(1, [P, PASSES, N], U32, "wd_codes")
+
+        wd_codes = staged(5 * SLOT + PACK * N * 4, [P, PASSES, N], U32, "wd_codes")
         nc.sync.dma_start(
             wd_codes[:].bitcast(I32), wd_words.rearrange("a p n i -> p a (n i)").bitcast(I32)
         )
-        kb_cols = staged(4, [P, N_TILES], F32, "kb_cols")
+        kb_cols = staged(4 * SLOT + PACK * N * 4, [P, N_TILES], F32, "kb_cols")
         with nc.allow_non_contiguous_dma(reason="one value of kb for each partition"):
             nc.sync.dma_start(kb_cols[:], kb.rearrange("(c p) -> p c", p=P))
         wn_codes = held([P, PASSES * N], U32, "wn_codes")
@@ -214,7 +235,7 @@ def tile_list_mixing_closure_kernel(
 
         def make_h(piece, b):
             lo, hi = OUT_CUTS[piece], OUT_CUTS[piece + 1]
-            h = work.tile([P, hi - lo, PACK], BF16, name=f"h{b}", align_bytes=64)
+            h = work.tile([P, hi - lo, PACK], BF16, name=f"h{b}", align_bytes=64, bufs=3)
             for jb in range(lo // JB, hi // JB):
                 bank = psum1.tile([P, PACK, JB], F32, name="bank1")
                 for a in range(PASSES):
@@ -229,8 +250,8 @@ def tile_list_mixing_closure_kernel(
 
         def quantize_h(h, b):
             width = h.shape[1]
-            codes = work.tile([P, width], U32, name=f"h_codes{b}", align_bytes=64)
-            plane = work.tile([P, width], U8, name=f"h_plane{b}", align_bytes=64)
+            codes = work.tile([P, width], U32, name=f"h_codes{b}", align_bytes=64, bufs=3)
+            plane = work.tile([P, width], U8, name=f"h_plane{b}", align_bytes=64, bufs=3)
             nc.vector.quantize_mx(
                 out=codes[:].bitcast(FP8X4), scales=plane[:], in_=h[:].rearrange("p j t -> p (j t)")
             )
@@ -272,30 +293,45 @@ def tile_list_mixing_closure_kernel(
         def finish(piece, num, recip):
             lo, hi = OUT_CUTS[piece], OUT_CUTS[piece + 1]
             shape = [P, N_TILES, hi - lo]
-            ratio = work.tile(shape, F32, name="ratio")
-            result = work.tile(shape, F32, name="result")
+            ratio = work.tile(shape, F32, name="ratio", bufs=3)
+            result = held(shape, F32, f"result{piece}")
             for rows, bank in num:
                 nc.vector.tensor_tensor(ratio[:, rows, :], bank[:], recip[:, rows, :], MULT)
             for c in range(N_TILES):
-                nc.scalar.activation(
-                    result[:, c, :], ratio[:, c, :], ACT.Identity, bias=kb_cols[:, c : c + 1]
-                )
+                if piece + 1 < len(OUT_CUTS) - 1:
+                    nc.gpsimd.tensor_scalar(
+                        result[:, c, :], ratio[:, c, :], 1.0, kb_cols[:, c : c + 1], MULT, ADD
+                    )
+                else:
+                    nc.vector.tensor_scalar(
+                        result[:, c, :], ratio[:, c, :], 1.0, kb_cols[:, c : c + 1], MULT, ADD
+                    )
             nc.sync.dma_start(out.rearrange("(c p) j -> p c j", p=P)[:, :, lo:hi], result[:])
 
         pieces = len(OUT_CUTS) - 1
         wd_flat = wd_codes[:].rearrange("p b n -> p (b n)")
         wd_plane_flat = wd_plane[:].rearrange("p b n -> p (b n)")
-        packed = [quantize_h(make_h(0, b), b) for b in range(PASSES)]
+        made = []
+        for b in range(PASSES):
+            made.append(make_h(0, b))
+            group_wn(b)
+            strat_banks([(0, 6 + b)])
+            strat_banks([(1, 6 + b)])
+        packed = [quantize_h(made[b], b) for b in range(PASSES)]
         quantize_wn()
         for piece in range(pieces):
             width = OUT_CUTS[piece + 1] - OUT_CUTS[piece]
             more = piece + 1 < pieces
             if more:
-                h_low = make_h(piece + 1, 0)
+                low = make_h(piece + 1, 0)
+            if piece + 2 == pieces:
+                high = make_h(piece + 1, 1)
+                following = [quantize_h(low, 0), quantize_h(high, 1)]
             den = second_stage(packed, wd_flat, wd_plane_flat, "den")
             recip = reciprocal_of_denominator(den, width)
             num = second_stage(packed, wn_codes, wn_plane, "num")
-            if more:
-                h_high = make_h(piece + 1, 1)
-                packed = [quantize_h(h_low, 0), quantize_h(h_high, 1)]
+            if piece + 2 < pieces:
+                high = make_h(piece + 1, 1)
+                following = [quantize_h(low, 0), quantize_h(high, 1)]
+            packed = following
             finish(piece, num, recip)

@@ -25,7 +25,7 @@ JB = 128
 BANK = 512
 SLOT = 8192
 N_TILES = N // P
-GATHER_CUTS = (0, 256, 512, 1024)
+GATHER_CUTS = (0, 512, 1024)
 OUT_CUTS = (0, 256, 512, 768, 896, 1024)
 
 
@@ -52,7 +52,7 @@ def tile_list_mixing_closure_kernel(
 
         tab_scale_win = held([P, T], U8, "tab_scale_win")
         nc.gpsimd.memset(tab_scale_win[:].bitcast(I32), 0)
-        wb_scale_raw = staged(7 * SLOT, [P, PASSES, H], U8, "wb_scale_raw")
+        wb_scale_raw = held([P, PASSES, H], U8, "wb_scale_raw")
         nc.vector.memset(wb_scale_raw[:].bitcast(I32), 0)
 
         warm = held([P, 1], F32, "warm")
@@ -125,50 +125,36 @@ def tile_list_mixing_closure_kernel(
                 v_codes[a][:, lo:hi], tab_win[a][:].indirect(offsets[:, lo // 16 : hi // 16])
             )
 
-        def first_stage_pass(bank, codes, plane, a, jb, code_dtype, code_cols):
-            js = slice(jb * JB, (jb + 1) * JB)
-            for t in range(PACK):
-                nc.tensor.matmul_mx(
-                    out=bank[:, t, :],
-                    lhsT=codes[:, t * code_cols : (t + 1) * code_cols].bitcast(code_dtype),
-                    lhsT_scale=plane[:, t * P : (t + 1) * P],
-                    rhs=v_codes[a][:, js].bitcast(FP8X4),
-                    rhs_scale=v_scales[a][:, js],
-                    start=(a == 0 and t == 0),
-                    stop=(a == PASSES - 1 and t == PACK - 1),
-                )
-
         strat = {}
 
-        def strat_banks(pairs, spare=()):
-            banks = [psum1.tile([P, PACK, JB], F32, name="bank1") for pair in pairs[len(spare) :]]
-            banks.extend(psum2.tile([P, PACK, JB], F32, name=name) for name in spare)
+        def strat_banks(half, blocks, spare=()):
+            js = slice(half * BANK, (half + 1) * BANK)
+            jobs = [(b, t) for b in blocks for t in range(PACK)]
+            banks = [psum1.tile([P, BANK], F32, name="bank1") for job in jobs[len(spare) :]]
+            banks.extend(psum2.tile([P, BANK], F32, name=name) for name in spare)
             for a in range(PASSES):
-                for bank, (b, jb) in zip(banks, pairs):
-                    first_stage_pass(bank, wb_codes[b][:, a, :], wb_plane[b][:, a, :], a, jb, FP4X4, 2 * P)
-            for bank, (b, jb) in zip(banks, pairs):
-                strat[b, jb] = held([P, JB, PACK], F32, f"strat{b}_{jb}")
-                nc.scalar.copy(strat[b, jb][:], bank[:].rearrange("p t j -> p j t"))
+                for bank, (b, t) in zip(banks, jobs):
+                    nc.tensor.matmul_mx(
+                        out=bank[:],
+                        lhsT=wb_codes[b][:, a, t * 2 * P : (t + 1) * 2 * P].bitcast(FP4X4),
+                        lhsT_scale=wb_plane[b][:, a, t * P : (t + 1) * P],
+                        rhs=v_codes[a][:, js].bitcast(FP8X4),
+                        rhs_scale=v_scales[a][:, js],
+                        start=(a == 0),
+                        stop=(a == PASSES - 1),
+                    )
+            for b in blocks:
+                strat[b, half] = held([P, PACK, BANK], F32, f"strat{b}_{half}")
+            for bank, (b, t) in zip(banks, jobs):
+                nc.scalar.copy(strat[b, half][:, t, :], bank[:])
 
         reorder_wb(0)
         gather_words(0, 0)
         reorder_wb(1)
-        wd_plane = staged(7 * SLOT, [P, PASSES, N], U8, "wd_plane")
-        nc.vector.memset(wd_plane[:].bitcast(I32), 0)
-        for d in range(4):
-            nc.gpsimd.dma_start(
-                wd_plane[32 * d : 32 * d + 4].bitcast(I32),
-                wd_scales[:, 4 * d : 4 * d + 4, :].rearrange("a c n -> c a n").bitcast(I32),
-            )
-        gather_words(0, 1)
         gather_words(1, 0)
-        gather_words(1, 1)
-        strat_banks(
-            [(0, 0), (0, 1), (1, 0), (1, 1), (0, 2), (1, 2), (0, 3), (1, 3)],
-            spare=("den", "den", "num", "num"),
-        )
+        strat_banks(0, (0, 1), spare=("den", "den", "num", "num"))
         for a in range(PASSES):
-            gather_words(a, 2)
+            gather_words(a, 1)
 
         ws_codes, ws_plane = {}, {}
 
@@ -195,9 +181,7 @@ def tile_list_mixing_closure_kernel(
         high = [group_ws(a, 1, nc.vector.tensor_copy) for a in range(PASSES)]
         for a in range(PASSES):
             quantize_ws(a, 1, high[a])
-        for jb in (4, 5):
-            for b in range(PASSES):
-                strat_banks([(b, jb)])
+        strat_banks(1, (0,))
 
         wn_grouped = held([P, PASSES * N * PACK], BF16, "wn_grouped")
         wn_raw = []
@@ -219,6 +203,13 @@ def tile_list_mixing_closure_kernel(
         nc.sync.dma_start(
             wd_codes[:].bitcast(I32), wd_words.rearrange("a p n i -> p a (n i)").bitcast(I32)
         )
+        wd_plane = staged(5 * SLOT - 1024, [P, PASSES, N], U8, "wd_plane")
+        nc.vector.memset(wd_plane[:].bitcast(I32), 0)
+        for d in range(4):
+            nc.sync.dma_start(
+                wd_plane[32 * d : 32 * d + 4].bitcast(I32),
+                wd_scales[:, 4 * d : 4 * d + 4, :].rearrange("a c n -> c a n").bitcast(I32),
+            )
         kb_cols = staged(4 * SLOT + PACK * N * 4, [P, N_TILES], F32, "kb_cols")
         with nc.allow_non_contiguous_dma(reason="one value of kb for each partition"):
             nc.sync.dma_start(kb_cols[:], kb.rearrange("(c p) -> p c", p=P))
@@ -238,12 +229,23 @@ def tile_list_mixing_closure_kernel(
             h = work.tile([P, hi - lo, PACK], BF16, name=f"h{b}", align_bytes=64, bufs=3)
             for jb in range(lo // JB, hi // JB):
                 bank = psum1.tile([P, PACK, JB], F32, name="bank1")
-                for a in range(PASSES):
-                    first_stage_pass(bank, ws_codes[a, b], ws_plane[a, b], a, jb, FP8X4, P)
+                js = slice(jb * JB, (jb + 1) * JB)
+                for t in range(PACK):
+                    for a in range(PASSES):
+                        nc.tensor.matmul_mx(
+                            out=bank[:, t, :],
+                            lhsT=ws_codes[a, b][:, t * P : (t + 1) * P].bitcast(FP8X4),
+                            lhsT_scale=ws_plane[a, b][:, t * P : (t + 1) * P],
+                            rhs=v_codes[a][:, js].bitcast(FP8X4),
+                            rhs_scale=v_scales[a][:, js],
+                            start=(a == 0),
+                            stop=(a == PASSES - 1),
+                        )
+                half, first = divmod(jb * JB, BANK)
                 nc.vector.tensor_tensor(
-                    h[:, jb * JB - lo : (jb + 1) * JB - lo, :],
-                    bank[:].rearrange("p t j -> p j t"),
-                    strat[b, jb][:],
+                    h[:, jb * JB - lo : (jb + 1) * JB - lo, :].rearrange("p (g i) t -> p g t i", i=4),
+                    bank[:].rearrange("p t (g i) -> p g t i", i=4),
+                    strat[b, half][:, :, first : first + JB].rearrange("p t (g i) -> p g t i", i=4),
                     MULT,
                 )
             return h
@@ -298,25 +300,19 @@ def tile_list_mixing_closure_kernel(
             for rows, bank in num:
                 nc.vector.tensor_tensor(ratio[:, rows, :], bank[:], recip[:, rows, :], MULT)
             for c in range(N_TILES):
-                if piece + 1 < len(OUT_CUTS) - 1:
-                    nc.gpsimd.tensor_scalar(
-                        result[:, c, :], ratio[:, c, :], 1.0, kb_cols[:, c : c + 1], MULT, ADD
-                    )
-                else:
-                    nc.vector.tensor_scalar(
-                        result[:, c, :], ratio[:, c, :], 1.0, kb_cols[:, c : c + 1], MULT, ADD
-                    )
+                nc.vector.tensor_scalar(
+                    result[:, c, :], ratio[:, c, :], 1.0, kb_cols[:, c : c + 1], MULT, ADD
+                )
             nc.sync.dma_start(out.rearrange("(c p) j -> p c j", p=P)[:, :, lo:hi], result[:])
 
         pieces = len(OUT_CUTS) - 1
         wd_flat = wd_codes[:].rearrange("p b n -> p (b n)")
         wd_plane_flat = wd_plane[:].rearrange("p b n -> p (b n)")
-        made = []
+        made = [make_h(0, 0)]
+        strat_banks(1, (1,), spare=("den", "den", "num", "num"))
+        made.append(make_h(0, 1))
         for b in range(PASSES):
-            made.append(make_h(0, b))
             group_wn(b)
-            strat_banks([(0, 6 + b)])
-            strat_banks([(1, 6 + b)])
         packed = [quantize_h(made[b], b) for b in range(PASSES)]
         quantize_wn()
         for piece in range(pieces):

@@ -24,6 +24,7 @@ PASSES = 2
 JB = 128
 BANK = 512
 SLOT = 8192
+WS_OFFSET = {(0, 0): 0, (1, 0): 6 * SLOT + 1024, (0, 1): 2 * SLOT, (1, 1): 3 * SLOT}
 N_TILES = N // P
 GATHER_CUTS = (0, 512, 1024)
 OUT_CUTS = (0, 256, 512, 768, 896, 1024)
@@ -50,7 +51,7 @@ def tile_list_mixing_closure_kernel(
         offsets = lists.tile([P, S // 16], U16, name="offsets")
         nc.sync.dma_start(offsets[:], offs)
 
-        tab_scale_win = held([P, T], U8, "tab_scale_win")
+        tab_scale_win = staged(6 * SLOT - 512, [P, T], U8, "tab_scale_win")
         nc.gpsimd.memset(tab_scale_win[:].bitcast(I32), 0)
         wb_scale_raw = held([P, PASSES, H], U8, "wb_scale_raw")
         nc.vector.memset(wb_scale_raw[:].bitcast(I32), 0)
@@ -62,29 +63,42 @@ def tile_list_mixing_closure_kernel(
         wb_raw = held([P, PASSES, 2 * H], U8, "wb_raw")
         nc.sync.dma_start(wb_raw[:].bitcast(I32), wb_words.rearrange("a p c -> p a c").bitcast(I32))
         for a in range(PASSES):
-            nc.sync.dma_start(tab_scale_win[a:P:8, :].bitcast(I32), tab_scales[a].bitcast(I32))
+            for i in range(2):
+                nc.sync.dma_start(
+                    tab_scale_win[2 * a + i : P : 16, :].bitcast(I32),
+                    tab_scales[a, i:16:2, :].bitcast(I32),
+                )
         v_scales = [held([P, S], U8, f"v_scales{a}") for a in range(PASSES)]
-        for d in range(4):
-            nc.sync.dma_start(
-                wb_scale_raw[32 * d : 32 * d + 4].bitcast(I32),
-                wb_scales[:, 4 * d : 4 * d + 4, :].rearrange("a c n -> c a n").bitcast(I32),
-            )
         ws_raw = {}
 
         def load_ws(a, b):
-            raw = staged((2 * b + a) * SLOT, [P, PACK, K_PASS], F32, f"ws_raw{a}{b}")
-            rows = ws[a * K_PASS : (a + 1) * K_PASS, b * K_PASS : (b + 1) * K_PASS]
-            nc.sync.dma_start(raw[:], rows.rearrange("(p i) r -> p i r", i=PACK))
-            ws_raw[a, b] = raw
+            parts = 2 if (a, b) == (1, 1) else 1
+            width = K_PASS // parts
+            ws_raw[a, b] = []
+            for part in range(parts):
+                offset = WS_OFFSET[a, b] + part * (SLOT // parts + 1024)
+                raw = staged(offset, [P, PACK, width], F32, f"ws_raw{a}{b}{part}")
+                first = b * K_PASS + part * width
+                rows = ws[a * K_PASS : (a + 1) * K_PASS, first : first + width]
+                nc.sync.dma_start(raw[:], rows.rearrange("(p i) r -> p i r", i=PACK))
+                ws_raw[a, b].append(raw)
 
         tab_win = []
-        for a in range(PASSES):
+
+        def load_table(a):
             win = staged((4 + a) * SLOT, [P, T], U32, f"tab_win{a}")
             nc.sync.dma_start(
                 win[:].bitcast(I32), tab_words[a].rearrange("p t i -> p (t i)").bitcast(I32)
             )
             tab_win.append(win)
-            load_ws(a, 0)
+
+        load_table(0)
+        for d in range(4):
+            nc.sync.dma_start(
+                wb_scale_raw[32 * d : 32 * d + 4].bitcast(I32),
+                wb_scales[:, 4 * d : 4 * d + 4, :].rearrange("a c n -> c a n").bitcast(I32),
+            )
+        load_ws(0, 0)
 
         nc.vector.memset(v_scales[1][:].bitcast(I32), 0)
 
@@ -93,13 +107,15 @@ def tile_list_mixing_closure_kernel(
         nc.vector.tensor_copy(v_scales[0][:].bitcast(I32), picked_scales[:].bitcast(I32))
         for a in range(PASSES):
             for c in range(4):
-                if (a, c) != (0, 0):
-                    queue = nc.gpsimd if (a, c) == (1, 3) else nc.scalar
-                    queue.dma_start(
+                row = 16 * (c // 2) + 2 * a + c % 2
+                if row != c:
+                    nc.sync.dma_start(
                         v_scales[a][c:P:32, :].bitcast(I32),
-                        picked_scales[8 * c + a : P : 32, :].bitcast(I32),
+                        picked_scales[row:P:32, :].bitcast(I32),
                     )
 
+        load_table(1)
+        load_ws(1, 0)
         for a in range(PASSES):
             load_ws(a, 1)
 
@@ -160,10 +176,12 @@ def tile_list_mixing_closure_kernel(
 
         def group_ws(a, b, copy):
             grouped = held([P, PACK, P, PACK], BF16, f"ws_grouped{a}{b}")
-            copy(
-                grouped[:].rearrange("p t m i -> p m t i"),
-                ws_raw[a, b][:].rearrange("p i (m t) -> p m t i", t=PACK),
-            )
+            count = P // len(ws_raw[a, b])
+            for part, raw in enumerate(ws_raw[a, b]):
+                copy(
+                    grouped[:, :, part * count : (part + 1) * count, :].rearrange("p t m i -> p m t i"),
+                    raw[:].rearrange("p i (m t) -> p m t i", t=PACK),
+                )
             return grouped
 
         def quantize_ws(a, b, grouped):
@@ -186,7 +204,7 @@ def tile_list_mixing_closure_kernel(
         wn_grouped = held([P, PASSES * N * PACK], BF16, "wn_grouped")
         wn_raw = []
         for b in range(PASSES):
-            raw = staged((4 + b) * SLOT, [P, PACK, N], F32, f"wn_raw{b}")
+            raw = staged((4 + b) * SLOT + (1 - b) * 1024, [P, PACK, N], F32, f"wn_raw{b}")
             rows = wn[b * K_PASS : (b + 1) * K_PASS, :]
             nc.sync.dma_start(raw[:], rows.rearrange("(p i) n -> p i n", i=PACK))
             wn_raw.append(raw)
@@ -210,7 +228,7 @@ def tile_list_mixing_closure_kernel(
                 wd_plane[32 * d : 32 * d + 4].bitcast(I32),
                 wd_scales[:, 4 * d : 4 * d + 4, :].rearrange("a c n -> c a n").bitcast(I32),
             )
-        kb_cols = staged(4 * SLOT + PACK * N * 4, [P, N_TILES], F32, "kb_cols")
+        kb_cols = staged(5 * SLOT - 128, [P, N_TILES], F32, "kb_cols")
         with nc.allow_non_contiguous_dma(reason="one value of kb for each partition"):
             nc.sync.dma_start(kb_cols[:], kb.rearrange("(c p) -> p c", p=P))
         wn_codes = held([P, PASSES * N], U32, "wn_codes")
@@ -300,7 +318,8 @@ def tile_list_mixing_closure_kernel(
             for rows, bank in num:
                 nc.vector.tensor_tensor(ratio[:, rows, :], bank[:], recip[:, rows, :], MULT)
             for c in range(N_TILES):
-                nc.vector.tensor_scalar(
+                engine = nc.vector if hi == S else nc.gpsimd
+                engine.tensor_scalar(
                     result[:, c, :], ratio[:, c, :], 1.0, kb_cols[:, c : c + 1], MULT, ADD
                 )
             nc.sync.dma_start(out.rearrange("(c p) j -> p c j", p=P)[:, :, lo:hi], result[:])

@@ -23,10 +23,9 @@ K_PASS = P * PACK
 PASSES = 2
 JB = 128
 BANK = 512
-SLOT = 8192
-WS_OFFSET = {(0, 0): 0, (1, 0): 6 * SLOT + 1024, (0, 1): 2 * SLOT, (1, 1): 3 * SLOT}
+LAP = 64
+WN_STEP = 96
 N_TILES = N // P
-GATHER_CUTS = (0, 512, 1024)
 OUT_CUTS = (0, 256, 512, 768, 896, 1024)
 
 
@@ -39,58 +38,67 @@ def tile_list_mixing_closure_kernel(
         keep = ctx.enter_context(tc.tile_pool(name="keep", bufs=1))
         stage = ctx.enter_context(tc.tile_pool(name="stage", bufs=1))
         work = ctx.enter_context(tc.tile_pool(name="work", bufs=2))
-        psum1 = ctx.enter_context(tc.psum_pool(name="psum1", bufs=4))
-        psum2 = ctx.enter_context(tc.psum_pool(name="psum2", bufs=2))
-
-        def staged(offset, shape, dtype, name):
-            return stage.tile(shape, dtype, name=name, offset=offset, align_bytes=64)
+        psum = ctx.enter_context(tc.psum_pool(name="psum", bufs=8))
 
         def held(shape, dtype, name):
             return keep.tile(shape, dtype, name=name, align_bytes=64)
 
+        place = {}
+        cursor = 0
+        for first, anchor, last in (
+            (("ws_raw10", 4 * T), ("tab_scale_win", T), ("tab_win1", 4 * T)),
+            (("ws_raw01", 4 * T), ("picked", S), ("ws_raw11", 4 * T)),
+            (("wd_plane", 2 * N), ("tab_win0", 4 * T), ("wd_codes", 8 * N)),
+            (("wn_raw0", 16 * N), ("ws_raw00", 4 * T), ("wn_raw1", 16 * N)),
+        ):
+            place[first[0]] = cursor
+            place[anchor[0]] = cursor + first[1] - LAP
+            place[last[0]] = place[anchor[0]] + anchor[1] - LAP
+            cursor = place[last[0]] + last[1]
+        place["ws_grouped01"] = place["wn_grouped"] = cursor
+        place["ws_grouped11"] = cursor + 2 * T
+
+        def staged(shape, dtype, name):
+            return stage.tile(shape, dtype, name=name, offset=place[name], align_bytes=64)
+
+        def new_bank():
+            return psum.tile([P, BANK], F32, name="bank")
+
         offsets = lists.tile([P, S // 16], U16, name="offsets")
         nc.sync.dma_start(offsets[:], offs)
 
-        tab_scale_win = staged(6 * SLOT - 512, [P, T], U8, "tab_scale_win")
+        tab_scale_win = staged([P, T], U8, "tab_scale_win")
         nc.gpsimd.memset(tab_scale_win[:].bitcast(I32), 0)
         wb_scale_raw = held([P, PASSES, H], U8, "wb_scale_raw")
         nc.vector.memset(wb_scale_raw[:].bitcast(I32), 0)
+        v_scales = held([P, PASSES, S], U8, "v_scales")
+        nc.vector.memset(v_scales[:].bitcast(I32), 0)
 
         warm = held([P, 1], F32, "warm")
         nc.vector.memset(warm[:], 1.0)
         nc.scalar.activation(warm[:], warm[:], ACT.Abs_reciprocal_sqrt)
 
-        wb_raw = held([P, PASSES, 2 * H], U8, "wb_raw")
-        nc.sync.dma_start(wb_raw[:].bitcast(I32), wb_words.rearrange("a p c -> p a c").bitcast(I32))
-        for a in range(PASSES):
-            for i in range(2):
-                nc.sync.dma_start(
-                    tab_scale_win[2 * a + i : P : 16, :].bitcast(I32),
-                    tab_scales[a, i:16:2, :].bitcast(I32),
-                )
-        v_scales = [held([P, S], U8, f"v_scales{a}") for a in range(PASSES)]
-        ws_raw = {}
-
-        def load_ws(a, b):
-            parts = 2 if (a, b) == (1, 1) else 1
-            width = K_PASS // parts
-            ws_raw[a, b] = []
-            for part in range(parts):
-                offset = WS_OFFSET[a, b] + part * (SLOT // parts + 1024)
-                raw = staged(offset, [P, PACK, width], F32, f"ws_raw{a}{b}{part}")
-                first = b * K_PASS + part * width
-                rows = ws[a * K_PASS : (a + 1) * K_PASS, first : first + width]
-                nc.sync.dma_start(raw[:], rows.rearrange("(p i) r -> p i r", i=PACK))
-                ws_raw[a, b].append(raw)
-
+        wb_raw = [held([P, 2 * H], U8, "wb_raw0"), held([P, 2 * H], U8, "wb_raw1")]
+        kb_cols = held([P, N_TILES], F32, "kb_cols")
+        with nc.allow_non_contiguous_dma(reason="one value of kb for each partition"):
+            nc.sync.dma_start(kb_cols[:], kb.rearrange("(c p) -> p c", p=P))
+        nc.sync.dma_start(
+            tab_scale_win[0:P:4, :].bitcast(I32), tab_scales.rearrange("a q t -> q a t").bitcast(I32)
+        )
+        nc.sync.dma_start(wb_raw[0][:].bitcast(I32), wb_words[0].bitcast(I32))
         tab_win = []
 
         def load_table(a):
-            win = staged((4 + a) * SLOT, [P, T], U32, f"tab_win{a}")
-            nc.sync.dma_start(
-                win[:].bitcast(I32), tab_words[a].rearrange("p t i -> p (t i)").bitcast(I32)
-            )
+            win = staged([P, T], U32, f"tab_win{a}")
+            nc.sync.dma_start(win[:].bitcast(I32), tab_words[a].rearrange("p t i -> p (t i)").bitcast(I32))
             tab_win.append(win)
+
+        ws_raw = {}
+
+        def load_ws(a, b):
+            ws_raw[a, b] = staged([P, PACK, K_PASS], F32, f"ws_raw{a}{b}")
+            rows = ws[a * K_PASS : (a + 1) * K_PASS, b * K_PASS : (b + 1) * K_PASS]
+            nc.sync.dma_start(ws_raw[a, b][:], rows.rearrange("(p i) r -> p i r", i=PACK))
 
         load_table(0)
         for d in range(4):
@@ -98,89 +106,78 @@ def tile_list_mixing_closure_kernel(
                 wb_scale_raw[32 * d : 32 * d + 4].bitcast(I32),
                 wb_scales[:, 4 * d : 4 * d + 4, :].rearrange("a c n -> c a n").bitcast(I32),
             )
+        nc.sync.dma_start(wb_raw[1][:].bitcast(I32), wb_words[1].bitcast(I32))
         load_ws(0, 0)
 
-        nc.vector.memset(v_scales[1][:].bitcast(I32), 0)
-
-        picked_scales = staged(3 * SLOT - S // 2, [P, S], U8, "picked_scales")
-        nc.vector.tensor_copy(picked_scales[:], tab_scale_win[:].indirect(offsets[:]))
-        nc.vector.tensor_copy(v_scales[0][:].bitcast(I32), picked_scales[:].bitcast(I32))
-        for a in range(PASSES):
-            for c in range(4):
-                row = 16 * (c // 2) + 2 * a + c % 2
-                if row != c:
-                    nc.sync.dma_start(
-                        v_scales[a][c:P:32, :].bitcast(I32),
-                        picked_scales[row:P:32, :].bitcast(I32),
-                    )
+        picked = staged([P, S], U8, "picked")
+        nc.vector.tensor_copy(picked[:], tab_scale_win[:].indirect(offsets[:]))
+        for d in range(4):
+            nc.sync.dma_start(
+                v_scales[32 * d : 32 * d + 4].bitcast(I32), picked[32 * d : 32 * d + 32 : 4, :].bitcast(I32)
+            )
 
         load_table(1)
         load_ws(1, 0)
         for a in range(PASSES):
             load_ws(a, 1)
 
-        wb_codes = [held([P, PASSES, 2 * K_PASS], U8, f"wb_codes{b}") for b in range(PASSES)]
-        wb_plane = [held([P, PASSES, K_PASS], U8, f"wb_plane{b}") for b in range(PASSES)]
+        wb_codes = [held([P, 2 * H], U8, f"wb_codes{a}") for a in range(PASSES)]
+        wb_plane = [held([P, H], U8, f"wb_plane{a}") for a in range(PASSES)]
 
-        def reorder_wb(b):
-            cols = slice(b * K_PASS, (b + 1) * K_PASS)
+        def deal_words(a):
             nc.vector.tensor_copy(
-                wb_codes[b][:].bitcast(U16).rearrange("p a (t g m) -> p a g t m", t=PACK, m=8),
-                wb_raw[:].bitcast(U16)[:, :, cols].rearrange("p a (g m t) -> p a g t m", t=PACK, m=8),
-            )
-            nc.vector.tensor_copy(
-                wb_plane[b][:].rearrange("p a (t g m) -> p a g t m", t=PACK, m=16),
-                wb_scale_raw[:, :, cols].rearrange("p a (g m t) -> p a g t m", t=PACK, m=16),
+                wb_codes[a][:].bitcast(U16).rearrange("p (b t g m) -> p b g t m", b=PASSES, t=PACK, m=8),
+                wb_raw[a][:].bitcast(U16).rearrange("p (b g m t) -> p b g t m", b=PASSES, t=PACK, m=8),
             )
 
-        v_codes = [held([P, S], U32, f"v_codes{a}") for a in range(PASSES)]
-
-        def gather_words(a, piece):
-            lo, hi = GATHER_CUTS[piece], GATHER_CUTS[piece + 1]
+        def deal_plane(a):
             nc.vector.tensor_copy(
-                v_codes[a][:, lo:hi], tab_win[a][:].indirect(offsets[:, lo // 16 : hi // 16])
+                wb_plane[a][:].rearrange("p (b t g m) -> p b g t m", b=PASSES, t=PACK, m=16),
+                wb_scale_raw[:, a, :].rearrange("p (b g m t) -> p b g t m", b=PASSES, t=PACK, m=16),
             )
+
+        v_codes = [[held([P, BANK], U32, f"v_codes{a}{half}") for half in range(2)] for a in range(PASSES)]
+
+        def gather_words(a, half):
+            cols = slice(half * BANK // 16, (half + 1) * BANK // 16)
+            nc.vector.tensor_copy(v_codes[a][half][:], tab_win[a][:].indirect(offsets[:, cols]))
 
         strat = {}
 
-        def strat_banks(half, blocks, spare=()):
+        def strat_banks(half, blocks):
             js = slice(half * BANK, (half + 1) * BANK)
             jobs = [(b, t) for b in blocks for t in range(PACK)]
-            banks = [psum1.tile([P, BANK], F32, name="bank1") for job in jobs[len(spare) :]]
-            banks.extend(psum2.tile([P, BANK], F32, name=name) for name in spare)
-            for a in range(PASSES):
-                for bank, (b, t) in zip(banks, jobs):
-                    nc.tensor.matmul_mx(
-                        out=bank[:],
-                        lhsT=wb_codes[b][:, a, t * 2 * P : (t + 1) * 2 * P].bitcast(FP4X4),
-                        lhsT_scale=wb_plane[b][:, a, t * P : (t + 1) * P],
-                        rhs=v_codes[a][:, js].bitcast(FP8X4),
-                        rhs_scale=v_scales[a][:, js],
-                        start=(a == 0),
-                        stop=(a == PASSES - 1),
-                    )
+            banks = [new_bank() for job in jobs]
+            order = [(a, x) for a in range(PASSES) for x in range(len(jobs))]
+            if half:
+                order = [(a, x) for x in range(len(jobs)) for a in range(PASSES)]
+            for a, x in order:
+                b, t = jobs[x]
+                col = (b * PACK + t) * P
+                nc.tensor.matmul_mx(
+                    out=banks[x][:],
+                    lhsT=wb_codes[a][:, 2 * col : 2 * (col + P)].bitcast(FP4X4),
+                    lhsT_scale=wb_plane[a][:, col : col + P],
+                    rhs=v_codes[a][half][:].bitcast(FP8X4),
+                    rhs_scale=v_scales[:, a, js],
+                    start=(a == 0),
+                    stop=(a == PASSES - 1),
+                )
             for b in blocks:
                 strat[b, half] = held([P, PACK, BANK], F32, f"strat{b}_{half}")
             for bank, (b, t) in zip(banks, jobs):
                 nc.scalar.copy(strat[b, half][:, t, :], bank[:])
 
-        reorder_wb(0)
-        gather_words(0, 0)
-        reorder_wb(1)
-        gather_words(1, 0)
-        strat_banks(0, (0, 1), spare=("den", "den", "num", "num"))
-        for a in range(PASSES):
-            gather_words(a, 1)
-
         ws_codes, ws_plane = {}, {}
 
-        def group_ws(a, b, copy):
-            grouped = held([P, PACK, P, PACK], BF16, f"ws_grouped{a}{b}")
-            count = P // len(ws_raw[a, b])
-            for part, raw in enumerate(ws_raw[a, b]):
+        def group_ws(a, b, copies):
+            grouped = (held, staged)[b]([P, PACK, P, PACK], BF16, f"ws_grouped{a}{b}")
+            count = P // len(copies)
+            for part, copy in enumerate(copies):
+                ms = slice(part * count, (part + 1) * count)
                 copy(
-                    grouped[:, :, part * count : (part + 1) * count, :].rearrange("p t m i -> p m t i"),
-                    raw[:].rearrange("p i (m t) -> p m t i", t=PACK),
+                    grouped[:, :, ms, :].rearrange("p t m i -> p m t i"),
+                    ws_raw[a, b][:].rearrange("p i (m t) -> p m t i", t=PACK)[:, ms],
                 )
             return grouped
 
@@ -193,44 +190,82 @@ def tile_list_mixing_closure_kernel(
                 in_=grouped[:].rearrange("p t m i -> p (t m i)"),
             )
 
-        low = [group_ws(0, 0, nc.scalar.copy), group_ws(1, 0, nc.vector.tensor_copy)]
+        deal_words(0)
+        gather_words(0, 0)
+        deal_plane(0)
+        low = [group_ws(0, 0, [nc.scalar.copy])]
+        deal_plane(1)
+        deal_words(1)
+        gather_words(1, 0)
+        strat_banks(0, (0, 1))
+        gather_words(0, 1)
+        gather_words(1, 1)
+        low.append(group_ws(1, 0, [nc.vector.tensor_copy]))
         for a in range(PASSES):
             quantize_ws(a, 0, low[a])
-        high = [group_ws(a, 1, nc.vector.tensor_copy) for a in range(PASSES)]
-        for a in range(PASSES):
-            quantize_ws(a, 1, high[a])
-        strat_banks(1, (0,))
 
-        wn_grouped = held([P, PASSES * N * PACK], BF16, "wn_grouped")
-        wn_raw = []
-        for b in range(PASSES):
-            raw = staged((4 + b) * SLOT + (1 - b) * 1024, [P, PACK, N], F32, f"wn_raw{b}")
-            rows = wn[b * K_PASS : (b + 1) * K_PASS, :]
-            nc.sync.dma_start(raw[:], rows.rearrange("(p i) n -> p i n", i=PACK))
-            wn_raw.append(raw)
+        pieces = len(OUT_CUTS) - 1
+        widths = [OUT_CUTS[x + 1] - OUT_CUTS[x] for x in range(pieces)]
+        h = [held([P, PASSES, widths[x], PACK], BF16, f"h{x}") for x in range(pieces)]
+        h_codes = [held([P, PASSES, widths[x]], U32, f"h_codes{x}") for x in range(pieces)]
+        h_plane = [held([P, PASSES, widths[x]], U8, f"h_plane{x}") for x in range(pieces)]
 
-        def group_wn(b):
-            nc.scalar.copy(
-                wn_grouped[:, b * N * PACK : (b + 1) * N * PACK].rearrange(
-                    "p (g n i) -> p g i n", n=4, i=PACK
-                ),
-                wn_raw[b][:].rearrange("p i (g n) -> p g i n", n=4),
+        def make_h(piece, b):
+            lo, hi = OUT_CUTS[piece], OUT_CUTS[piece + 1]
+            for jb in range(lo // JB, hi // JB):
+                bank = new_bank()[:].rearrange("p (t j) -> p t j", t=PACK)
+                half, first = divmod(jb * JB, BANK)
+                for t in range(PACK):
+                    for a in range(PASSES):
+                        nc.tensor.matmul_mx(
+                            out=bank[:, t, :],
+                            lhsT=ws_codes[a, b][:, t * P : (t + 1) * P].bitcast(FP8X4),
+                            lhsT_scale=ws_plane[a, b][:, t * P : (t + 1) * P],
+                            rhs=v_codes[a][half][:, first : first + JB].bitcast(FP8X4),
+                            rhs_scale=v_scales[:, a, jb * JB : (jb + 1) * JB],
+                            start=(a == 0),
+                            stop=(a == PASSES - 1),
+                        )
+                nc.vector.tensor_tensor(
+                    h[piece][:, b, jb * JB - lo : (jb + 1) * JB - lo, :].rearrange("p (g i) t -> p g t i", i=4),
+                    bank.rearrange("p t (g i) -> p g t i", i=4),
+                    strat[b, half][:, :, first : first + JB].rearrange("p t (g i) -> p g t i", i=4),
+                    MULT,
+                )
+
+        def quantize_h(piece, blocks):
+            nc.vector.quantize_mx(
+                out=h_codes[piece][:, blocks, :].rearrange("p b j -> p (b j)").bitcast(FP8X4),
+                scales=h_plane[piece][:, blocks, :].rearrange("p b j -> p (b j)"),
+                in_=h[piece][:, blocks].rearrange("p b j t -> p (b j t)"),
             )
 
-        wd_codes = staged(5 * SLOT + PACK * N * 4, [P, PASSES, N], U32, "wd_codes")
-        nc.sync.dma_start(
-            wd_codes[:].bitcast(I32), wd_words.rearrange("a p n i -> p a (n i)").bitcast(I32)
-        )
-        wd_plane = staged(5 * SLOT - 1024, [P, PASSES, N], U8, "wd_plane")
-        nc.vector.memset(wd_plane[:].bitcast(I32), 0)
+
+        wd_codes = staged([P, PASSES, N], U32, "wd_codes")
+        nc.sync.dma_start(wd_codes[:].bitcast(I32), wd_words.rearrange("a p n i -> p a (n i)").bitcast(I32))
+        wd_plane = staged([P, PASSES, N], U8, "wd_plane")
+        nc.gpsimd.memset(wd_plane[:].bitcast(I32), 0)
         for d in range(4):
             nc.sync.dma_start(
                 wd_plane[32 * d : 32 * d + 4].bitcast(I32),
                 wd_scales[:, 4 * d : 4 * d + 4, :].rearrange("a c n -> c a n").bitcast(I32),
             )
-        kb_cols = staged(5 * SLOT - 128, [P, N_TILES], F32, "kb_cols")
-        with nc.allow_non_contiguous_dma(reason="one value of kb for each partition"):
-            nc.sync.dma_start(kb_cols[:], kb.rearrange("(c p) -> p c", p=P))
+
+        wn_raw = []
+        for b in range(PASSES):
+            wn_raw.append(staged([P, PACK, N], F32, f"wn_raw{b}"))
+            nc.sync.dma_start(wn_raw[b][:], wn[b * K_PASS : (b + 1) * K_PASS, :].rearrange("(p i) n -> p i n", i=PACK))
+
+        def group_wn():
+            grouped = staged([P, PASSES, N, PACK], BF16, "wn_grouped")
+            for b in range(PASSES):
+                for first in range(0, N, WN_STEP):
+                    ns = slice(first, first + WN_STEP)
+                    nc.gpsimd.tensor_scalar(
+                        grouped[:, b, ns, :], wn_raw[b][:, :, ns].rearrange("p i n -> p n i"), 1.0, 0.0, MULT, ADD
+                    )
+            return grouped[:].rearrange("p b n i -> p (b n i)")
+
         wn_codes = held([P, PASSES * N], U32, "wn_codes")
         wn_plane = held([P, PASSES * N], U8, "wn_plane")
 
@@ -242,48 +277,13 @@ def tile_list_mixing_closure_kernel(
                     in_=wn_grouped[:, PACK * lo : PACK * hi],
                 )
 
-        def make_h(piece, b):
-            lo, hi = OUT_CUTS[piece], OUT_CUTS[piece + 1]
-            h = work.tile([P, hi - lo, PACK], BF16, name=f"h{b}", align_bytes=64, bufs=3)
-            for jb in range(lo // JB, hi // JB):
-                bank = psum1.tile([P, PACK, JB], F32, name="bank1")
-                js = slice(jb * JB, (jb + 1) * JB)
-                for t in range(PACK):
-                    for a in range(PASSES):
-                        nc.tensor.matmul_mx(
-                            out=bank[:, t, :],
-                            lhsT=ws_codes[a, b][:, t * P : (t + 1) * P].bitcast(FP8X4),
-                            lhsT_scale=ws_plane[a, b][:, t * P : (t + 1) * P],
-                            rhs=v_codes[a][:, js].bitcast(FP8X4),
-                            rhs_scale=v_scales[a][:, js],
-                            start=(a == 0),
-                            stop=(a == PASSES - 1),
-                        )
-                half, first = divmod(jb * JB, BANK)
-                nc.vector.tensor_tensor(
-                    h[:, jb * JB - lo : (jb + 1) * JB - lo, :].rearrange("p (g i) t -> p g t i", i=4),
-                    bank[:].rearrange("p t (g i) -> p g t i", i=4),
-                    strat[b, half][:, :, first : first + JB].rearrange("p t (g i) -> p g t i", i=4),
-                    MULT,
-                )
-            return h
-
-        def quantize_h(h, b):
-            width = h.shape[1]
-            codes = work.tile([P, width], U32, name=f"h_codes{b}", align_bytes=64, bufs=3)
-            plane = work.tile([P, width], U8, name=f"h_plane{b}", align_bytes=64, bufs=3)
-            nc.vector.quantize_mx(
-                out=codes[:].bitcast(FP8X4), scales=plane[:], in_=h[:].rearrange("p j t -> p (j t)")
-            )
-            return codes, plane
-
-        def second_stage(packed, codes, plane, name):
-            width = packed[0][0].shape[1]
+        def second_stage(piece, codes, plane):
+            width = widths[piece]
             per_bank = min(N_TILES, BANK // width)
             banks = []
             for first in range(0, N_TILES, per_bank):
                 rows = range(first, min(first + per_bank, N_TILES))
-                bank = psum2.tile([P, len(rows), width], F32, name=name)
+                bank = new_bank()[:, : len(rows) * width].rearrange("p (c j) -> p c j", j=width)
                 for c in rows:
                     for b in range(PASSES):
                         cols = slice(b * N + c * P, b * N + (c + 1) * P)
@@ -291,8 +291,8 @@ def tile_list_mixing_closure_kernel(
                             out=bank[:, c - first, :],
                             lhsT=codes[:, cols].bitcast(FP8X4),
                             lhsT_scale=plane[:, cols],
-                            rhs=packed[b][0][:].bitcast(FP8X4),
-                            rhs_scale=packed[b][1][:],
+                            rhs=h_codes[piece][:, b, :].bitcast(FP8X4),
+                            rhs_scale=h_plane[piece][:, b, :],
                             start=(b == 0),
                             stop=(b == PASSES - 1),
                         )
@@ -303,9 +303,9 @@ def tile_list_mixing_closure_kernel(
             shape = [P, N_TILES, width]
             den_sq = work.tile(shape, F32, name="den_sq")
             root = work.tile(shape, F32, name="root")
-            recip = work.tile(shape, F32, name="recip")
+            recip = work.tile(shape, F32, name="recip", bufs=5)
             for rows, bank in den:
-                nc.scalar.activation(den_sq[:, rows, :], bank[:], ACT.Square)
+                nc.scalar.activation(den_sq[:, rows, :], bank, ACT.Square)
             nc.scalar.activation(root[:], den_sq[:], ACT.Abs_reciprocal_sqrt, bias=1.0)
             nc.scalar.activation(recip[:], root[:], ACT.Square)
             return recip
@@ -316,37 +316,52 @@ def tile_list_mixing_closure_kernel(
             ratio = work.tile(shape, F32, name="ratio", bufs=3)
             result = held(shape, F32, f"result{piece}")
             for rows, bank in num:
-                nc.vector.tensor_tensor(ratio[:, rows, :], bank[:], recip[:, rows, :], MULT)
+                nc.vector.tensor_tensor(ratio[:, rows, :], bank, recip[:, rows, :], MULT)
             for c in range(N_TILES):
                 engine = nc.vector if hi == S else nc.gpsimd
-                engine.tensor_scalar(
-                    result[:, c, :], ratio[:, c, :], 1.0, kb_cols[:, c : c + 1], MULT, ADD
-                )
+                engine.tensor_scalar(result[:, c, :], ratio[:, c, :], 1.0, kb_cols[:, c : c + 1], MULT, ADD)
             nc.sync.dma_start(out.rearrange("(c p) j -> p c j", p=P)[:, :, lo:hi], result[:])
 
-        pieces = len(OUT_CUTS) - 1
         wd_flat = wd_codes[:].rearrange("p b n -> p (b n)")
         wd_plane_flat = wd_plane[:].rearrange("p b n -> p (b n)")
-        made = [make_h(0, 0)]
-        strat_banks(1, (1,), spare=("den", "den", "num", "num"))
-        made.append(make_h(0, 1))
-        for b in range(PASSES):
-            group_wn(b)
-        packed = [quantize_h(made[b], b) for b in range(PASSES)]
+        recips = {}
+        both = slice(0, PASSES)
+
+        def denominator(piece):
+            recips[piece] = reciprocal_of_denominator(second_stage(piece, wd_flat, wd_plane_flat), widths[piece])
+
+        def numerator(piece):
+            finish(piece, second_stage(piece, wn_codes, wn_plane), recips[piece])
+
+        high = [group_ws(0, 1, [nc.vector.tensor_copy])]
+        make_h(0, 0)
+        high.append(group_ws(1, 1, [nc.vector.tensor_copy]))
+        for a in range(PASSES):
+            quantize_ws(a, 1, high[a])
+        wn_grouped = group_wn()
+        make_h(1, 0)
+        strat_banks(1, (0, 1))
+        make_h(0, 1)
+        quantize_h(0, both)
+        make_h(1, 1)
+        quantize_h(1, both)
+        denominator(0)
+        make_h(2, 0)
         quantize_wn()
-        for piece in range(pieces):
-            width = OUT_CUTS[piece + 1] - OUT_CUTS[piece]
-            more = piece + 1 < pieces
-            if more:
-                low = make_h(piece + 1, 0)
-            if piece + 2 == pieces:
-                high = make_h(piece + 1, 1)
-                following = [quantize_h(low, 0), quantize_h(high, 1)]
-            den = second_stage(packed, wd_flat, wd_plane_flat, "den")
-            recip = reciprocal_of_denominator(den, width)
-            num = second_stage(packed, wn_codes, wn_plane, "num")
-            if piece + 2 < pieces:
-                high = make_h(piece + 1, 1)
-                following = [quantize_h(low, 0), quantize_h(high, 1)]
-            packed = following
-            finish(piece, num, recip)
+        denominator(1)
+        make_h(2, 1)
+        quantize_h(2, both)
+        numerator(0)
+        make_h(3, 0)
+        make_h(3, 1)
+        quantize_h(3, both)
+        denominator(2)
+        make_h(4, 0)
+        make_h(4, 1)
+        quantize_h(4, both)
+        numerator(1)
+        denominator(3)
+        denominator(4)
+        numerator(2)
+        numerator(3)
+        numerator(4)

@@ -24,7 +24,6 @@ PASSES = 2
 JB = 128
 BANK = 512
 LAP = 64
-WN_STEP = 96
 N_TILES = N // P
 OUT_CUTS = (0, 256, 512, 768, 896, 1024)
 
@@ -38,7 +37,7 @@ def tile_list_mixing_closure_kernel(
         keep = ctx.enter_context(tc.tile_pool(name="keep", bufs=1))
         stage = ctx.enter_context(tc.tile_pool(name="stage", bufs=1))
         work = ctx.enter_context(tc.tile_pool(name="work", bufs=2))
-        psum = ctx.enter_context(tc.psum_pool(name="psum", bufs=8))
+        psum = ctx.enter_context(tc.psum_pool(name="psum", bufs=1))
 
         def held(shape, dtype, name):
             return keep.tile(shape, dtype, name=name, align_bytes=64)
@@ -55,14 +54,16 @@ def tile_list_mixing_closure_kernel(
             place[anchor[0]] = cursor + first[1] - LAP
             place[last[0]] = place[anchor[0]] + anchor[1] - LAP
             cursor = place[last[0]] + last[1]
-        place["ws_grouped01"] = place["wn_grouped"] = cursor
-        place["ws_grouped11"] = cursor + 2 * T
+        place["h0"] = place["ws_raw01"] + LAP
+        place["ws_grouped11"] = place["h1"] = cursor
 
         def staged(shape, dtype, name):
             return stage.tile(shape, dtype, name=name, offset=place[name], align_bytes=64)
 
+        bank_order = list(range(PACK)) + list(range(8)) * 8
+
         def new_bank():
-            return psum.tile([P, BANK], F32, name="bank")
+            return psum.tile([P, BANK], F32, name=f"bank{bank_order.pop(0)}")
 
         offsets = lists.tile([P, S // 16], U16, name="offsets")
         nc.sync.dma_start(offsets[:], offs)
@@ -149,7 +150,7 @@ def tile_list_mixing_closure_kernel(
             jobs = [(b, t) for b in blocks for t in range(PACK)]
             banks = [new_bank() for job in jobs]
             order = [(a, x) for a in range(PASSES) for x in range(len(jobs))]
-            if half:
+            if half or blocks[0]:
                 order = [(a, x) for x in range(len(jobs)) for a in range(PASSES)]
             for a, x in order:
                 b, t = jobs[x]
@@ -171,7 +172,7 @@ def tile_list_mixing_closure_kernel(
         ws_codes, ws_plane = {}, {}
 
         def group_ws(a, b, copies):
-            grouped = (held, staged)[b]([P, PACK, P, PACK], BF16, f"ws_grouped{a}{b}")
+            grouped = (staged if a + b == 2 else held)([P, PACK, P, PACK], BF16, f"ws_grouped{a}{b}")
             count = P // len(copies)
             for part, copy in enumerate(copies):
                 ms = slice(part * count, (part + 1) * count)
@@ -197,7 +198,8 @@ def tile_list_mixing_closure_kernel(
         deal_plane(1)
         deal_words(1)
         gather_words(1, 0)
-        strat_banks(0, (0, 1))
+        strat_banks(0, (0,))
+        strat_banks(0, (1,))
         gather_words(0, 1)
         gather_words(1, 1)
         low.append(group_ws(1, 0, [nc.vector.tensor_copy]))
@@ -206,7 +208,7 @@ def tile_list_mixing_closure_kernel(
 
         pieces = len(OUT_CUTS) - 1
         widths = [OUT_CUTS[x + 1] - OUT_CUTS[x] for x in range(pieces)]
-        h = [held([P, PASSES, widths[x], PACK], BF16, f"h{x}") for x in range(pieces)]
+        h = [(staged if x < 2 else held)([P, PASSES, widths[x], PACK], BF16, f"h{x}") for x in range(pieces)]
         h_codes = [held([P, PASSES, widths[x]], U32, f"h_codes{x}") for x in range(pieces)]
         h_plane = [held([P, PASSES, widths[x]], U8, f"h_plane{x}") for x in range(pieces)]
 
@@ -257,13 +259,12 @@ def tile_list_mixing_closure_kernel(
             nc.sync.dma_start(wn_raw[b][:], wn[b * K_PASS : (b + 1) * K_PASS, :].rearrange("(p i) n -> p i n", i=PACK))
 
         def group_wn():
-            grouped = staged([P, PASSES, N, PACK], BF16, "wn_grouped")
+            grouped = held([P, PASSES, N, PACK], BF16, "wn_grouped")
             for b in range(PASSES):
-                for first in range(0, N, WN_STEP):
-                    ns = slice(first, first + WN_STEP)
-                    nc.gpsimd.tensor_scalar(
-                        grouped[:, b, ns, :], wn_raw[b][:, :, ns].rearrange("p i n -> p n i"), 1.0, 0.0, MULT, ADD
-                    )
+                nc.scalar.copy(
+                    grouped[:, b].rearrange("p (g n) i -> p g i n", n=4),
+                    wn_raw[b][:].rearrange("p i (g n) -> p g i n", n=4),
+                )
             return grouped[:].rearrange("p b n i -> p (b n i)")
 
         wn_codes = held([P, PASSES * N], U32, "wn_codes")
@@ -338,9 +339,9 @@ def tile_list_mixing_closure_kernel(
         high.append(group_ws(1, 1, [nc.vector.tensor_copy]))
         for a in range(PASSES):
             quantize_ws(a, 1, high[a])
-        wn_grouped = group_wn()
         make_h(1, 0)
         strat_banks(1, (0, 1))
+        wn_grouped = group_wn()
         make_h(0, 1)
         quantize_h(0, both)
         make_h(1, 1)

@@ -54,6 +54,7 @@ def tile_list_mixing_closure_kernel(
             place[anchor[0]] = cursor + first[1] - LAP
             place[last[0]] = place[anchor[0]] + anchor[1] - LAP
             cursor = place[last[0]] + last[1]
+        place["kb_cols"] = place["tab_win1"] + 4 * T - LAP
         place["h0"] = place["ws_raw01"] + LAP
         place["ws_grouped11"] = place["h1"] = cursor
 
@@ -80,9 +81,6 @@ def tile_list_mixing_closure_kernel(
         nc.scalar.activation(warm[:], warm[:], ACT.Abs_reciprocal_sqrt)
 
         wb_raw = [held([P, 2 * H], U8, "wb_raw0"), held([P, 2 * H], U8, "wb_raw1")]
-        kb_cols = held([P, N_TILES], F32, "kb_cols")
-        with nc.allow_non_contiguous_dma(reason="one value of kb for each partition"):
-            nc.sync.dma_start(kb_cols[:], kb.rearrange("(c p) -> p c", p=P))
         nc.sync.dma_start(
             tab_scale_win[0:P:4, :].bitcast(I32), tab_scales.rearrange("a q t -> q a t").bitcast(I32)
         )
@@ -177,8 +175,8 @@ def tile_list_mixing_closure_kernel(
             for part, copy in enumerate(copies):
                 ms = slice(part * count, (part + 1) * count)
                 copy(
-                    grouped[:, :, ms, :].rearrange("p t m i -> p m t i"),
-                    ws_raw[a, b][:].rearrange("p i (m t) -> p m t i", t=PACK)[:, ms],
+                    grouped[:, :, ms, :].rearrange("p (u e) m i -> p m u i e", e=2),
+                    ws_raw[a, b][:].rearrange("p i (m u e) -> p m u i e", u=2, e=2)[:, ms],
                 )
             return grouped
 
@@ -229,9 +227,9 @@ def tile_list_mixing_closure_kernel(
                             stop=(a == PASSES - 1),
                         )
                 nc.vector.tensor_tensor(
-                    h[piece][:, b, jb * JB - lo : (jb + 1) * JB - lo, :].rearrange("p (g i) t -> p g t i", i=4),
-                    bank.rearrange("p t (g i) -> p g t i", i=4),
-                    strat[b, half][:, :, first : first + JB].rearrange("p t (g i) -> p g t i", i=4),
+                    h[piece][:, b, jb * JB - lo : (jb + 1) * JB - lo, :].rearrange("p (g i) t -> p g t i", i=2),
+                    bank.rearrange("p t (g i) -> p g t i", i=2),
+                    strat[b, half][:, :, first : first + JB].rearrange("p t (g i) -> p g t i", i=2),
                     MULT,
                 )
 
@@ -253,6 +251,9 @@ def tile_list_mixing_closure_kernel(
                 wd_scales[:, 4 * d : 4 * d + 4, :].rearrange("a c n -> c a n").bitcast(I32),
             )
 
+        kb_cols = staged([P, N_TILES], F32, "kb_cols")
+        with nc.allow_non_contiguous_dma(reason="one value of kb for each partition"):
+            nc.sync.dma_start(kb_cols[:], kb.rearrange("(c p) -> p c", p=P))
         wn_raw = []
         for b in range(PASSES):
             wn_raw.append(staged([P, PACK, N], F32, f"wn_raw{b}"))
@@ -262,8 +263,8 @@ def tile_list_mixing_closure_kernel(
             grouped = held([P, PASSES, N, PACK], BF16, "wn_grouped")
             for b in range(PASSES):
                 nc.scalar.copy(
-                    grouped[:, b].rearrange("p (g n) i -> p g i n", n=4),
-                    wn_raw[b][:].rearrange("p i (g n) -> p g i n", n=4),
+                    grouped[:, b].rearrange("p (g n) i -> p g i n", n=2),
+                    wn_raw[b][:].rearrange("p i (g n) -> p g i n", n=2),
                 )
             return grouped[:].rearrange("p b n i -> p (b n i)")
 

@@ -24,6 +24,8 @@ PASSES = 2
 JB = 128
 BANK = 512
 LAP = 64
+VECTOR_ADDS_FROM = 768
+WN_STEP = 96
 N_TILES = N // P
 OUT_CUTS = (0, 256, 512, 768, 896, 1024)
 
@@ -45,23 +47,26 @@ def tile_list_mixing_closure_kernel(
         place = {}
         cursor = 0
         for first, anchor, last in (
-            (("ws_raw10", 4 * T), ("tab_scale_win", T), ("tab_win1", 4 * T)),
+            (("ws_raw10", 4 * T), ("tab_scale_win", T), ("ws_raw00", 4 * T)),
             (("ws_raw01", 4 * T), ("picked", S), ("ws_raw11", 4 * T)),
-            (("wd_plane", 2 * N), ("tab_win0", 4 * T), ("wd_codes", 8 * N)),
-            (("wn_raw0", 16 * N), ("ws_raw00", 4 * T), ("wn_raw1", 16 * N)),
+            (("wd_plane", 2 * N), ("wb_scale_raw", 2 * H), ("kb_cols", 2 * LAP)),
+            (("wd_codes", 8 * N), ("tab_win0", 4 * T), ("h0", 0)),
+            (("wn_raw0", 16 * N), ("tab_win1", 4 * T), ("wn_raw1", 16 * N)),
         ):
             place[first[0]] = cursor
             place[anchor[0]] = cursor + first[1] - LAP
             place[last[0]] = place[anchor[0]] + anchor[1] - LAP
             cursor = place[last[0]] + last[1]
-        place["kb_cols"] = place["tab_win1"] + 4 * T - LAP
-        place["h0"] = place["ws_raw01"] + LAP
-        place["ws_grouped11"] = place["h1"] = cursor
+        place["strat0_1"] = place["ws_raw01"] + LAP
+        place["ws_grouped11"] = place["h1"] = cursor + LAP
+        place["wn_grouped"] = place["h1"] + 2 * T - LAP
+        place["h1"] = cursor
 
         def staged(shape, dtype, name):
             return stage.tile(shape, dtype, name=name, offset=place[name], align_bytes=64)
 
-        bank_order = list(range(PACK)) + list(range(8)) * 8
+        low_banks, high_banks = list(range(4)), list(range(4, 8))
+        bank_order = (2 * low_banks + high_banks) * 2 + (low_banks + high_banks) * 4
 
         def new_bank():
             return psum.tile([P, BANK], F32, name=f"bank{bank_order.pop(0)}")
@@ -71,7 +76,7 @@ def tile_list_mixing_closure_kernel(
 
         tab_scale_win = staged([P, T], U8, "tab_scale_win")
         nc.gpsimd.memset(tab_scale_win[:].bitcast(I32), 0)
-        wb_scale_raw = held([P, PASSES, H], U8, "wb_scale_raw")
+        wb_scale_raw = staged([P, PASSES, H], U8, "wb_scale_raw")
         nc.vector.memset(wb_scale_raw[:].bitcast(I32), 0)
         v_scales = held([P, PASSES, S], U8, "v_scales")
         nc.vector.memset(v_scales[:].bitcast(I32), 0)
@@ -106,7 +111,7 @@ def tile_list_mixing_closure_kernel(
                 wb_scales[:, 4 * d : 4 * d + 4, :].rearrange("a c n -> c a n").bitcast(I32),
             )
         nc.sync.dma_start(wb_raw[1][:].bitcast(I32), wb_words[1].bitcast(I32))
-        load_ws(0, 0)
+        load_table(1)
 
         picked = staged([P, S], U8, "picked")
         nc.vector.tensor_copy(picked[:], tab_scale_win[:].indirect(offsets[:]))
@@ -115,7 +120,7 @@ def tile_list_mixing_closure_kernel(
                 v_scales[32 * d : 32 * d + 4].bitcast(I32), picked[32 * d : 32 * d + 32 : 4, :].bitcast(I32)
             )
 
-        load_table(1)
+        load_ws(0, 0)
         load_ws(1, 0)
         for a in range(PASSES):
             load_ws(a, 1)
@@ -130,9 +135,9 @@ def tile_list_mixing_closure_kernel(
             )
 
         def deal_plane(a):
-            nc.vector.tensor_copy(
-                wb_plane[a][:].rearrange("p (b t g m) -> p b g t m", b=PASSES, t=PACK, m=16),
-                wb_scale_raw[:, a, :].rearrange("p (b g m t) -> p b g t m", b=PASSES, t=PACK, m=16),
+            nc.gpsimd.tensor_copy(
+                wb_plane[a][:].rearrange("p (b t m) -> p b t m", b=PASSES, t=PACK),
+                wb_scale_raw[:, a, :].rearrange("p (b m t) -> p b t m", b=PASSES, t=PACK),
             )
 
         v_codes = [[held([P, BANK], U32, f"v_codes{a}{half}") for half in range(2)] for a in range(PASSES)]
@@ -163,7 +168,7 @@ def tile_list_mixing_closure_kernel(
                     stop=(a == PASSES - 1),
                 )
             for b in blocks:
-                strat[b, half] = held([P, PACK, BANK], F32, f"strat{b}_{half}")
+                strat[b, half] = (staged if (b, half) == (0, 1) else held)([P, PACK, BANK], F32, f"strat{b}_{half}")
             for bank, (b, t) in zip(banks, jobs):
                 nc.scalar.copy(strat[b, half][:, t, :], bank[:])
 
@@ -192,7 +197,6 @@ def tile_list_mixing_closure_kernel(
         deal_words(0)
         gather_words(0, 0)
         deal_plane(0)
-        low = [group_ws(0, 0, [nc.scalar.copy])]
         deal_plane(1)
         deal_words(1)
         gather_words(1, 0)
@@ -200,13 +204,13 @@ def tile_list_mixing_closure_kernel(
         strat_banks(0, (1,))
         gather_words(0, 1)
         gather_words(1, 1)
-        low.append(group_ws(1, 0, [nc.vector.tensor_copy]))
+        low = [group_ws(a, 0, [nc.vector.tensor_copy]) for a in range(PASSES)]
         for a in range(PASSES):
             quantize_ws(a, 0, low[a])
 
         pieces = len(OUT_CUTS) - 1
         widths = [OUT_CUTS[x + 1] - OUT_CUTS[x] for x in range(pieces)]
-        h = [(staged if x < 2 else held)([P, PASSES, widths[x], PACK], BF16, f"h{x}") for x in range(pieces)]
+        h = [(staged if x == 1 else held)([P, PASSES, widths[x], PACK], BF16, f"h{x}") for x in range(pieces)]
         h_codes = [held([P, PASSES, widths[x]], U32, f"h_codes{x}") for x in range(pieces)]
         h_plane = [held([P, PASSES, widths[x]], U8, f"h_plane{x}") for x in range(pieces)]
 
@@ -260,12 +264,13 @@ def tile_list_mixing_closure_kernel(
             nc.sync.dma_start(wn_raw[b][:], wn[b * K_PASS : (b + 1) * K_PASS, :].rearrange("(p i) n -> p i n", i=PACK))
 
         def group_wn():
-            grouped = held([P, PASSES, N, PACK], BF16, "wn_grouped")
+            grouped = staged([P, PASSES, N, PACK], BF16, "wn_grouped")
             for b in range(PASSES):
-                nc.scalar.copy(
-                    grouped[:, b].rearrange("p (g n) i -> p g i n", n=2),
-                    wn_raw[b][:].rearrange("p i (g n) -> p g i n", n=2),
-                )
+                for first in range(0, N, WN_STEP):
+                    ns = slice(first, first + WN_STEP)
+                    nc.gpsimd.tensor_scalar(
+                        grouped[:, b, ns, :], wn_raw[b][:, :, ns].rearrange("p i n -> p n i"), 1.0, 0.0, MULT, ADD
+                    )
             return grouped[:].rearrange("p b n i -> p (b n i)")
 
         wn_codes = held([P, PASSES * N], U32, "wn_codes")
@@ -319,9 +324,11 @@ def tile_list_mixing_closure_kernel(
             result = held(shape, F32, f"result{piece}")
             for rows, bank in num:
                 nc.vector.tensor_tensor(ratio[:, rows, :], bank, recip[:, rows, :], MULT)
-            for c in range(N_TILES):
-                engine = nc.vector if hi == S else nc.gpsimd
-                engine.tensor_scalar(result[:, c, :], ratio[:, c, :], 1.0, kb_cols[:, c : c + 1], MULT, ADD)
+            if lo >= VECTOR_ADDS_FROM:
+                nc.vector.tensor_tensor(result[:], ratio[:], kb_cols[:].unsqueeze(2).to_broadcast(shape), ADD)
+            else:
+                for c in range(N_TILES):
+                    nc.gpsimd.tensor_scalar(result[:, c, :], ratio[:, c, :], 1.0, kb_cols[:, c : c + 1], MULT, ADD)
             nc.sync.dma_start(out.rearrange("(c p) j -> p c j", p=P)[:, :, lo:hi], result[:])
 
         wd_flat = wd_codes[:].rearrange("p b n -> p (b n)")
@@ -335,7 +342,7 @@ def tile_list_mixing_closure_kernel(
         def numerator(piece):
             finish(piece, second_stage(piece, wn_codes, wn_plane), recips[piece])
 
-        high = [group_ws(0, 1, [nc.vector.tensor_copy])]
+        high = [group_ws(0, 1, [nc.scalar.copy])]
         make_h(0, 0)
         high.append(group_ws(1, 1, [nc.vector.tensor_copy]))
         for a in range(PASSES):
@@ -349,11 +356,10 @@ def tile_list_mixing_closure_kernel(
         quantize_h(1, both)
         denominator(0)
         make_h(2, 0)
-        quantize_wn()
         denominator(1)
         make_h(2, 1)
         quantize_h(2, both)
-        numerator(0)
+        quantize_wn()
         make_h(3, 0)
         make_h(3, 1)
         quantize_h(3, both)
@@ -361,9 +367,10 @@ def tile_list_mixing_closure_kernel(
         make_h(4, 0)
         make_h(4, 1)
         quantize_h(4, both)
-        numerator(1)
+        numerator(0)
         denominator(3)
         denominator(4)
+        numerator(1)
         numerator(2)
         numerator(3)
         numerator(4)

@@ -24,7 +24,7 @@ PASSES = 2
 JB = 128
 BANK = 512
 LAP = 64
-VECTOR_ADDS_FROM = 768
+SCALAR_ADDS_FROM = 512
 WN_STEP = 96
 N_TILES = N // P
 OUT_CUTS = (0, 256, 512, 768, 896, 1024)
@@ -46,17 +46,15 @@ def tile_list_mixing_closure_kernel(
 
         place = {}
         cursor = 0
-        for first, anchor, last in (
-            (("ws_raw10", 4 * T), ("tab_scale_win", T), ("ws_raw00", 4 * T)),
-            (("ws_raw01", 4 * T), ("picked", S), ("ws_raw11", 4 * T)),
-            (("wd_plane", 2 * N), ("wb_scale_raw", 2 * H), ("kb_cols", 2 * LAP)),
-            (("wd_codes", 8 * N), ("tab_win0", 4 * T), ("h0", 0)),
+        for chain in (
+            (("wd_codes", 8 * N), ("ws_raw10", 4 * T), ("tab_scale_win", T), ("ws_raw00", 4 * T), ("wd_plane", 2 * N)),
+            (("ws_raw01", 4 * T), ("picked", S), ("ws_raw11", 4 * T), ("kb_cols", 2 * LAP)),
             (("wn_raw0", 16 * N), ("tab_win1", 4 * T), ("wn_raw1", 16 * N)),
         ):
-            place[first[0]] = cursor
-            place[anchor[0]] = cursor + first[1] - LAP
-            place[last[0]] = place[anchor[0]] + anchor[1] - LAP
-            cursor = place[last[0]] + last[1]
+            for name, size in chain:
+                place[name] = cursor
+                cursor += size - LAP
+            cursor += LAP
         place["strat0_1"] = place["ws_raw01"] + LAP
         place["ws_grouped11"] = place["h1"] = cursor + LAP
         place["wn_grouped"] = place["h1"] + 2 * T - LAP
@@ -65,8 +63,8 @@ def tile_list_mixing_closure_kernel(
         def staged(shape, dtype, name):
             return stage.tile(shape, dtype, name=name, offset=place[name], align_bytes=64)
 
-        low_banks, high_banks = list(range(4)), list(range(4, 8))
-        bank_order = (2 * low_banks + high_banks) * 2 + (low_banks + high_banks) * 4
+        pairs = [0, 1, 2, 3, 0, 1, 2, 1, 0, 3, 1, 2] + [0, 3, 1, 2] * 6
+        bank_order = [2 * pair + x for pair in pairs for x in range(2)]
 
         def new_bank():
             return psum.tile([P, BANK], F32, name=f"bank{bank_order.pop(0)}")
@@ -76,7 +74,7 @@ def tile_list_mixing_closure_kernel(
 
         tab_scale_win = staged([P, T], U8, "tab_scale_win")
         nc.gpsimd.memset(tab_scale_win[:].bitcast(I32), 0)
-        wb_scale_raw = staged([P, PASSES, H], U8, "wb_scale_raw")
+        wb_scale_raw = held([P, PASSES, H], U8, "wb_scale_raw")
         nc.vector.memset(wb_scale_raw[:].bitcast(I32), 0)
         v_scales = held([P, PASSES, S], U8, "v_scales")
         nc.vector.memset(v_scales[:].bitcast(I32), 0)
@@ -93,7 +91,7 @@ def tile_list_mixing_closure_kernel(
         tab_win = []
 
         def load_table(a):
-            win = staged([P, T], U32, f"tab_win{a}")
+            win = (held, staged)[a]([P, T], U32, f"tab_win{a}")
             nc.sync.dma_start(win[:].bitcast(I32), tab_words[a].rearrange("p t i -> p (t i)").bitcast(I32))
             tab_win.append(win)
 
@@ -147,30 +145,34 @@ def tile_list_mixing_closure_kernel(
             nc.vector.tensor_copy(v_codes[a][half][:], tab_win[a][:].indirect(offsets[:, cols]))
 
         strat = {}
+        for half in range(2):
+            for b in range(PASSES):
+                strat[b, half] = None
 
-        def strat_banks(half, blocks):
-            js = slice(half * BANK, (half + 1) * BANK)
-            jobs = [(b, t) for b in blocks for t in range(PACK)]
-            banks = [new_bank() for job in jobs]
-            order = [(a, x) for a in range(PASSES) for x in range(len(jobs))]
-            if half or blocks[0]:
-                order = [(a, x) for x in range(len(jobs)) for a in range(PASSES)]
-            for a, x in order:
-                b, t = jobs[x]
-                col = (b * PACK + t) * P
-                nc.tensor.matmul_mx(
-                    out=banks[x][:],
-                    lhsT=wb_codes[a][:, 2 * col : 2 * (col + P)].bitcast(FP4X4),
-                    lhsT_scale=wb_plane[a][:, col : col + P],
-                    rhs=v_codes[a][half][:].bitcast(FP8X4),
-                    rhs_scale=v_scales[:, a, js],
-                    start=(a == 0),
-                    stop=(a == PASSES - 1),
-                )
-            for b in blocks:
-                strat[b, half] = (staged if (b, half) == (0, 1) else held)([P, PACK, BANK], F32, f"strat{b}_{half}")
-            for bank, (b, t) in zip(banks, jobs):
-                nc.scalar.copy(strat[b, half][:, t, :], bank[:])
+        def strat_pass(bank, half, b, t, a):
+            col = (b * PACK + t) * P
+            nc.tensor.matmul_mx(
+                out=bank[:],
+                lhsT=wb_codes[a][:, 2 * col : 2 * (col + P)].bitcast(FP4X4),
+                lhsT_scale=wb_plane[a][:, col : col + P],
+                rhs=v_codes[a][half][:].bitcast(FP8X4),
+                rhs_scale=v_scales[:, a, half * BANK : (half + 1) * BANK],
+                start=(a == 0),
+                stop=(a == PASSES - 1),
+            )
+
+        def strat_banks(half, b, slots, by_pass=False):
+            if strat[b, half] is None:
+                make = staged if (b, half) == (0, 1) else held
+                strat[b, half] = make([P, PACK, BANK], F32, f"strat{b}_{half}")
+            banks = {t: new_bank() for t in slots}
+            order = [(t, a) for t in slots for a in range(PASSES)]
+            if by_pass:
+                order = [(t, a) for a in range(PASSES) for t in slots]
+            for t, a in order:
+                strat_pass(banks[t], half, b, t, a)
+            for t in slots:
+                nc.scalar.copy(strat[b, half][:, t, :], banks[t][:])
 
         ws_codes, ws_plane = {}, {}
 
@@ -200,8 +202,8 @@ def tile_list_mixing_closure_kernel(
         deal_plane(1)
         deal_words(1)
         gather_words(1, 0)
-        strat_banks(0, (0,))
-        strat_banks(0, (1,))
+        strat_banks(0, 0, range(PACK), by_pass=True)
+        strat_banks(0, 1, range(PACK))
         gather_words(0, 1)
         gather_words(1, 1)
         low = [group_ws(a, 0, [nc.vector.tensor_copy]) for a in range(PASSES)]
@@ -324,7 +326,10 @@ def tile_list_mixing_closure_kernel(
             result = held(shape, F32, f"result{piece}")
             for rows, bank in num:
                 nc.vector.tensor_tensor(ratio[:, rows, :], bank, recip[:, rows, :], MULT)
-            if lo >= VECTOR_ADDS_FROM:
+            if lo >= SCALAR_ADDS_FROM and hi < S:
+                for c in range(N_TILES):
+                    nc.scalar.activation(result[:, c, :], ratio[:, c, :], ACT.Identity, bias=kb_cols[:, c : c + 1])
+            elif hi == S:
                 nc.vector.tensor_tensor(result[:], ratio[:], kb_cols[:].unsqueeze(2).to_broadcast(shape), ADD)
             else:
                 for c in range(N_TILES):
@@ -343,26 +348,29 @@ def tile_list_mixing_closure_kernel(
             finish(piece, second_stage(piece, wn_codes, wn_plane), recips[piece])
 
         high = [group_ws(0, 1, [nc.scalar.copy])]
+        strat_banks(1, 0, (0, 1))
         make_h(0, 0)
         high.append(group_ws(1, 1, [nc.vector.tensor_copy]))
         for a in range(PASSES):
             quantize_ws(a, 1, high[a])
         make_h(1, 0)
-        strat_banks(1, (0, 1))
         wn_grouped = group_wn()
+        strat_banks(1, 0, (2, 3))
+        strat_banks(1, 1, (0, 1))
         make_h(0, 1)
         quantize_h(0, both)
         make_h(1, 1)
         quantize_h(1, both)
-        denominator(0)
+        strat_banks(1, 1, (2, 3))
         make_h(2, 0)
-        denominator(1)
+        denominator(0)
         make_h(2, 1)
         quantize_h(2, both)
-        quantize_wn()
+        denominator(1)
         make_h(3, 0)
         make_h(3, 1)
         quantize_h(3, both)
+        quantize_wn()
         denominator(2)
         make_h(4, 0)
         make_h(4, 1)

@@ -24,7 +24,7 @@ PASSES = 2
 JB = 128
 BANK = 512
 LAP = 64
-SCALAR_ADDS_FROM = 512
+VECTOR_ADDS_FROM = 768
 WN_STEP = 96
 N_TILES = N // P
 OUT_CUTS = (0, 256, 512, 768, 896, 1024)
@@ -56,14 +56,14 @@ def tile_list_mixing_closure_kernel(
                 cursor += size - LAP
             cursor += LAP
         place["strat0_1"] = place["ws_raw01"] + LAP
-        place["ws_grouped11"] = place["h1"] = cursor + LAP
-        place["wn_grouped"] = place["h1"] + 2 * T - LAP
-        place["h1"] = cursor
+        place["strat0_0"] = cursor
+        place["ws_grouped11"] = cursor + 4 * T - LAP
+        place["wn_grouped"] = place["ws_grouped11"] + 2 * T - LAP
 
         def staged(shape, dtype, name):
             return stage.tile(shape, dtype, name=name, offset=place[name], align_bytes=64)
 
-        pairs = [0, 1, 2, 3, 0, 1, 2, 1, 0, 3, 1, 2] + [0, 3, 1, 2] * 6
+        pairs = [0, 1, 2, 3, 0, 1, 2, 1, 0, 2, 3, 1] + [0, 2, 3, 1] * 6
         bank_order = [2 * pair + x for pair in pairs for x in range(2)]
 
         def new_bank():
@@ -163,7 +163,7 @@ def tile_list_mixing_closure_kernel(
 
         def strat_banks(half, b, slots, by_pass=False):
             if strat[b, half] is None:
-                make = staged if (b, half) == (0, 1) else held
+                make = held if b else staged
                 strat[b, half] = make([P, PACK, BANK], F32, f"strat{b}_{half}")
             banks = {t: new_bank() for t in slots}
             order = [(t, a) for t in slots for a in range(PASSES)]
@@ -212,7 +212,7 @@ def tile_list_mixing_closure_kernel(
 
         pieces = len(OUT_CUTS) - 1
         widths = [OUT_CUTS[x + 1] - OUT_CUTS[x] for x in range(pieces)]
-        h = [(staged if x == 1 else held)([P, PASSES, widths[x], PACK], BF16, f"h{x}") for x in range(pieces)]
+        h = [held([P, PASSES, widths[x], PACK], BF16, f"h{x}") for x in range(pieces)]
         h_codes = [held([P, PASSES, widths[x]], U32, f"h_codes{x}") for x in range(pieces)]
         h_plane = [held([P, PASSES, widths[x]], U8, f"h_plane{x}") for x in range(pieces)]
 
@@ -326,10 +326,7 @@ def tile_list_mixing_closure_kernel(
             result = held(shape, F32, f"result{piece}")
             for rows, bank in num:
                 nc.vector.tensor_tensor(ratio[:, rows, :], bank, recip[:, rows, :], MULT)
-            if lo >= SCALAR_ADDS_FROM and hi < S:
-                for c in range(N_TILES):
-                    nc.scalar.activation(result[:, c, :], ratio[:, c, :], ACT.Identity, bias=kb_cols[:, c : c + 1])
-            elif hi == S:
+            if lo >= VECTOR_ADDS_FROM:
                 nc.vector.tensor_tensor(result[:], ratio[:], kb_cols[:].unsqueeze(2).to_broadcast(shape), ADD)
             else:
                 for c in range(N_TILES):
@@ -350,35 +347,34 @@ def tile_list_mixing_closure_kernel(
         high = [group_ws(0, 1, [nc.scalar.copy])]
         strat_banks(1, 0, (0, 1))
         make_h(0, 0)
+        make_h(1, 0)
         high.append(group_ws(1, 1, [nc.vector.tensor_copy]))
         for a in range(PASSES):
             quantize_ws(a, 1, high[a])
-        make_h(1, 0)
         wn_grouped = group_wn()
         strat_banks(1, 0, (2, 3))
-        strat_banks(1, 1, (0, 1))
+        strat_banks(1, 1, range(PACK))
         make_h(0, 1)
         quantize_h(0, both)
         make_h(1, 1)
         quantize_h(1, both)
-        strat_banks(1, 1, (2, 3))
         make_h(2, 0)
         denominator(0)
         make_h(2, 1)
         quantize_h(2, both)
         denominator(1)
+        quantize_wn()
         make_h(3, 0)
         make_h(3, 1)
         quantize_h(3, both)
-        quantize_wn()
+        numerator(0)
         denominator(2)
         make_h(4, 0)
         make_h(4, 1)
         quantize_h(4, both)
-        numerator(0)
+        numerator(1)
         denominator(3)
         denominator(4)
-        numerator(1)
         numerator(2)
         numerator(3)
         numerator(4)

@@ -24,6 +24,7 @@ PASSES = 2
 JB = 128
 BANK = 512
 LAP = 64
+WARM_PASSES = 3
 VECTOR_ADDS_FROM = 768
 WN_STEP = 96
 N_TILES = N // P
@@ -199,6 +200,17 @@ def tile_list_mixing_closure_kernel(
         deal_words(0)
         gather_words(0, 0)
         deal_plane(0)
+        idle_bank = psum.tile([P, BANK], F32, name="bank7")
+        for x in range(WARM_PASSES):
+            nc.tensor.matmul_mx(
+                out=idle_bank[:],
+                lhsT=wb_codes[0][:, : 2 * P].bitcast(FP4X4),
+                lhsT_scale=wb_plane[0][:, :P],
+                rhs=v_codes[0][0][:].bitcast(FP8X4),
+                rhs_scale=picked[:, :BANK],
+                start=True,
+                stop=True,
+            )
         deal_plane(1)
         deal_words(1)
         gather_words(1, 0)

@@ -76,9 +76,9 @@ def tile_list_mixing_closure_kernel(
         tab_scale_win = staged([P, T], U8, "tab_scale_win")
         nc.gpsimd.memset(tab_scale_win[:].bitcast(I32), 0)
         wb_scale_raw = held([P, PASSES, H], U8, "wb_scale_raw")
-        nc.vector.memset(wb_scale_raw[:].bitcast(I32), 0)
+        nc.gpsimd.memset(wb_scale_raw[:].bitcast(I32), 0)
         v_scales = held([P, PASSES, S], U8, "v_scales")
-        nc.vector.memset(v_scales[:].bitcast(I32), 0)
+        nc.gpsimd.memset(v_scales[:].bitcast(I32), 0)
 
         warm = held([P, 1], F32, "warm")
         nc.vector.memset(warm[:], 1.0)

@@ -128,10 +128,12 @@ def tile_list_mixing_closure_kernel(
         wb_plane = [held([P, H], U8, f"wb_plane{a}") for a in range(PASSES)]
 
         def deal_words(a):
-            nc.vector.tensor_copy(
-                wb_codes[a][:].bitcast(U16).rearrange("p (b t g m) -> p b g t m", b=PASSES, t=PACK, m=8),
-                wb_raw[a][:].bitcast(U16).rearrange("p (b g m t) -> p b g t m", b=PASSES, t=PACK, m=8),
-            )
+            for b in range(PASSES):
+                cols = slice(b * H, (b + 1) * H)
+                nc.gpsimd.tensor_copy(
+                    wb_codes[a][:, cols].rearrange("p (t m e) -> p t m e", t=PACK, e=2),
+                    wb_raw[a][:, cols].rearrange("p (m t e) -> p t m e", t=PACK, e=2),
+                )
 
         def deal_plane(a):
             nc.gpsimd.tensor_copy(

@@ -23,6 +23,7 @@ K_PASS = P * PACK
 PASSES = 2
 JB = 128
 BANK = 512
+WIDE = 256
 LAP = 64
 WARM_PASSES = 3
 VECTOR_ADDS_FROM = 768
@@ -152,30 +153,41 @@ def tile_list_mixing_closure_kernel(
             for b in range(PASSES):
                 strat[b, half] = None
 
-        def strat_pass(bank, half, b, t, a):
-            col = (b * PACK + t) * P
+        def strat_pass(bank, half, b, slot, e, a, start, stop):
+            quarter, u = divmod(slot, 2)
+            col = (b * PACK + 2 * u + e) * P
+            first = quarter * WIDE
             nc.tensor.matmul_mx(
-                out=bank[:],
+                out=bank[:, e, :],
                 lhsT=wb_codes[a][:, 2 * col : 2 * (col + P)].bitcast(FP4X4),
                 lhsT_scale=wb_plane[a][:, col : col + P],
-                rhs=v_codes[a][half][:].bitcast(FP8X4),
-                rhs_scale=v_scales[:, a, half * BANK : (half + 1) * BANK],
-                start=(a == 0),
-                stop=(a == PASSES - 1),
+                rhs=v_codes[a][half][:, first : first + WIDE].bitcast(FP8X4),
+                rhs_scale=v_scales[:, a, half * BANK + first : half * BANK + first + WIDE],
+                start=start,
+                stop=stop,
             )
 
         def strat_banks(half, b, slots, by_pass=False):
             if strat[b, half] is None:
                 make = held if b else staged
-                strat[b, half] = make([P, PACK, BANK], F32, f"strat{b}_{half}")
-            banks = {t: new_bank() for t in slots}
-            order = [(t, a) for t in slots for a in range(PASSES)]
+                strat[b, half] = make([P, 2, BANK, 2], F32, f"strat{b}_{half}")
+            banks = {slot: new_bank()[:].rearrange("p (e j) -> p e j", e=2) for slot in slots}
             if by_pass:
-                order = [(t, a) for a in range(PASSES) for t in slots]
-            for t, a in order:
-                strat_pass(banks[t], half, b, t, a)
-            for t in slots:
-                nc.scalar.copy(strat[b, half][:, t, :], banks[t][:])
+                for a in range(PASSES):
+                    for slot in slots:
+                        for e in range(2):
+                            strat_pass(banks[slot], half, b, slot, e, a, a + e == 0, a + e == 2)
+            else:
+                for slot in slots:
+                    for e in range(2):
+                        for a in range(PASSES):
+                            strat_pass(banks[slot], half, b, slot, e, a, a == 0, a == PASSES - 1)
+            for slot in slots:
+                quarter, u = divmod(slot, 2)
+                nc.scalar.copy(
+                    strat[b, half][:, u, quarter * WIDE : (quarter + 1) * WIDE, :],
+                    banks[slot].rearrange("p e j -> p j e"),
+                )
 
         ws_codes, ws_plane = {}, {}
 
@@ -247,9 +259,9 @@ def tile_list_mixing_closure_kernel(
                             stop=(a == PASSES - 1),
                         )
                 nc.vector.tensor_tensor(
-                    h[piece][:, b, jb * JB - lo : (jb + 1) * JB - lo, :].rearrange("p (g i) t -> p g t i", i=2),
-                    bank.rearrange("p t (g i) -> p g t i", i=2),
-                    strat[b, half][:, :, first : first + JB].rearrange("p t (g i) -> p g t i", i=2),
+                    h[piece][:, b, jb * JB - lo : (jb + 1) * JB - lo, :].rearrange("p j (u e) -> p j u e", e=2),
+                    bank.rearrange("p (u e) j -> p j u e", e=2),
+                    strat[b, half][:, :, first : first + JB, :].rearrange("p u j e -> p j u e"),
                     MULT,
                 )
 

@@ -341,8 +341,11 @@ def tile_list_mixing_closure_kernel(
             recip = work.tile(shape, F32, name="recip", bufs=5)
             for rows, bank in den:
                 nc.scalar.activation(den_sq[:, rows, :], bank, ACT.Square)
-            nc.scalar.activation(root[:], den_sq[:], ACT.Abs_reciprocal_sqrt, bias=1.0)
-            nc.scalar.activation(recip[:], root[:], ACT.Square)
+            halves = (slice(0, 2), slice(2, 3))
+            for rows in halves:
+                nc.scalar.activation(root[:, rows, :], den_sq[:, rows, :], ACT.Abs_reciprocal_sqrt, bias=1.0)
+            for rows in halves:
+                nc.scalar.activation(recip[:, rows, :], root[:, rows, :], ACT.Square)
             return recip
 
         def finish(piece, num, recip):

@@ -57,16 +57,17 @@ def tile_list_mixing_closure_kernel(
                 place[name] = cursor
                 cursor += size - LAP
             cursor += LAP
-        place["strat0_1"] = place["ws_raw01"] + LAP
-        place["strat0_0"] = cursor
-        place["ws_grouped11"] = cursor + 4 * T - LAP
+        place["strat0_3"] = place["ws_raw01"] + 2 * T - LAP - LAP + 2 * LAP
+        place["strat0_2"] = place["ws_raw01"]
+        place["strat0_1"] = cursor
+        place["ws_grouped11"] = cursor + 2 * T - LAP
         place["wn_grouped"] = place["ws_grouped11"] + 2 * T - LAP
 
         def staged(shape, dtype, name):
             return stage.tile(shape, dtype, name=name, offset=place[name], align_bytes=64)
 
-        pairs = [0, 1, 2, 3, 0, 1, 2, 1, 0, 2, 3, 1] + [0, 2, 3, 1] * 6
-        bank_order = [2 * pair + x for pair in pairs for x in range(2)]
+        pairs = [0, 1, 2, 3, 0, 1, 2, 1, 0, 2, 3, 1] + [0, 2, 3, 1] * 2 + [0]
+        bank_order = [2 * pair + x for pair in pairs for x in range(2)] + [4, 6, 7, 5, 2, 3, 0, 1]
 
         def new_bank():
             return psum.tile([P, BANK], F32, name=f"bank{bank_order.pop(0)}")
@@ -105,17 +106,16 @@ def tile_list_mixing_closure_kernel(
             nc.sync.dma_start(ws_raw[a, b][:], rows.rearrange("(p i) r -> p i r", i=PACK))
 
         load_table(0)
-        for d in range(4):
+        for c in range(4):
             nc.sync.dma_start(
-                wb_scale_raw[32 * d : 32 * d + 4].bitcast(I32),
-                wb_scales[:, 4 * d : 4 * d + 4, :].rearrange("a c n -> c a n").bitcast(I32),
+                wb_scale_raw[c:P:32].bitcast(I32), wb_scales[:, c:16:4, :].rearrange("a d n -> d a n").bitcast(I32)
             )
         nc.sync.dma_start(wb_raw[1][:].bitcast(I32), wb_words[1].bitcast(I32))
         load_table(1)
 
         picked = staged([P, S], U8, "picked")
         nc.vector.tensor_copy(picked[:], tab_scale_win[:].indirect(offsets[:]))
-        for d in range(4):
+        for d in (0, 2, 1, 3):
             nc.sync.dma_start(
                 v_scales[32 * d : 32 * d + 4].bitcast(I32), picked[32 * d : 32 * d + 32 : 4, :].bitcast(I32)
             )
@@ -149,9 +149,6 @@ def tile_list_mixing_closure_kernel(
             nc.vector.tensor_copy(v_codes[a][half][:], tab_win[a][:].indirect(offsets[:, cols]))
 
         strat = {}
-        for half in range(2):
-            for b in range(PASSES):
-                strat[b, half] = None
 
         def strat_pass(bank, half, b, slot, e, a, start, stop):
             quarter, u = divmod(slot, 2)
@@ -168,9 +165,9 @@ def tile_list_mixing_closure_kernel(
             )
 
         def strat_banks(half, b, slots, by_pass=False):
-            if strat[b, half] is None:
-                make = held if b else staged
-                strat[b, half] = make([P, 2, BANK, 2], F32, f"strat{b}_{half}")
+            for quarter in sorted({2 * half + slot // 2 for slot in slots}):
+                name = f"strat{b}_{quarter}"
+                strat[b, quarter] = (staged if name in place else held)([P, 2, WIDE, 2], F32, name)
             banks = {slot: new_bank()[:].rearrange("p (e j) -> p e j", e=2) for slot in slots}
             if by_pass:
                 for a in range(PASSES):
@@ -184,10 +181,7 @@ def tile_list_mixing_closure_kernel(
                             strat_pass(banks[slot], half, b, slot, e, a, a == 0, a == PASSES - 1)
             for slot in slots:
                 quarter, u = divmod(slot, 2)
-                nc.scalar.copy(
-                    strat[b, half][:, u, quarter * WIDE : (quarter + 1) * WIDE, :],
-                    banks[slot].rearrange("p e j -> p j e"),
-                )
+                nc.scalar.copy(strat[b, 2 * half + quarter][:, u], banks[slot].rearrange("p e j -> p j e"))
 
         ws_codes, ws_plane = {}, {}
 
@@ -261,7 +255,7 @@ def tile_list_mixing_closure_kernel(
                 nc.vector.tensor_tensor(
                     h[piece][:, b, jb * JB - lo : (jb + 1) * JB - lo, :].rearrange("p j (u e) -> p j u e", e=2),
                     bank.rearrange("p (u e) j -> p j u e", e=2),
-                    strat[b, half][:, :, first : first + JB, :].rearrange("p u j e -> p j u e"),
+                    strat[b, jb // 2][:, :, jb % 2 * JB : (jb % 2 + 1) * JB, :].rearrange("p u j e -> p j u e"),
                     MULT,
                 )
 
@@ -277,10 +271,9 @@ def tile_list_mixing_closure_kernel(
         nc.sync.dma_start(wd_codes[:].bitcast(I32), wd_words.rearrange("a p n i -> p a (n i)").bitcast(I32))
         wd_plane = staged([P, PASSES, N], U8, "wd_plane")
         nc.gpsimd.memset(wd_plane[:].bitcast(I32), 0)
-        for d in range(4):
+        for c in range(4):
             nc.sync.dma_start(
-                wd_plane[32 * d : 32 * d + 4].bitcast(I32),
-                wd_scales[:, 4 * d : 4 * d + 4, :].rearrange("a c n -> c a n").bitcast(I32),
+                wd_plane[c:P:32].bitcast(I32), wd_scales[:, c:16:4, :].rearrange("a d n -> d a n").bitcast(I32)
             )
 
         kb_cols = staged([P, N_TILES], F32, "kb_cols")
@@ -314,7 +307,7 @@ def tile_list_mixing_closure_kernel(
 
         def second_stage(piece, codes, plane):
             width = widths[piece]
-            per_bank = min(N_TILES, BANK // width)
+            per_bank = 2 if piece == pieces - 1 else min(N_TILES, BANK // width)
             banks = []
             for first in range(0, N_TILES, per_bank):
                 rows = range(first, min(first + per_bank, N_TILES))
@@ -353,6 +346,15 @@ def tile_list_mixing_closure_kernel(
             shape = [P, N_TILES, hi - lo]
             ratio = work.tile(shape, F32, name="ratio", bufs=3)
             result = held(shape, F32, f"result{piece}")
+            rows_out = out.rearrange("(c p) j -> p c j", p=P)
+            if piece == pieces - 1:
+                for rows, bank in num:
+                    nc.vector.tensor_tensor(ratio[:, rows, :], bank, recip[:, rows, :], MULT)
+                for rows, bank in num:
+                    for c in range(rows.start, rows.stop):
+                        nc.vector.tensor_scalar(result[:, c, :], ratio[:, c, :], kb_cols[:, c : c + 1], None, ADD)
+                    nc.sync.dma_start(rows_out[:, rows, lo:hi], result[:, rows, :])
+                return
             for rows, bank in num:
                 nc.vector.tensor_tensor(ratio[:, rows, :], bank, recip[:, rows, :], MULT)
             if lo >= VECTOR_ADDS_FROM:
@@ -360,6 +362,10 @@ def tile_list_mixing_closure_kernel(
             else:
                 for c in range(N_TILES):
                     nc.gpsimd.tensor_scalar(result[:, c, :], ratio[:, c, :], 1.0, kb_cols[:, c : c + 1], MULT, ADD)
+                    if hi == VECTOR_ADDS_FROM:
+                        nc.sync.dma_start(rows_out[:, c, lo:hi], result[:, c, :])
+                if hi == VECTOR_ADDS_FROM:
+                    return
             nc.sync.dma_start(out.rearrange("(c p) j -> p c j", p=P)[:, :, lo:hi], result[:])
 
         wd_flat = wd_codes[:].rearrange("p b n -> p (b n)")
@@ -403,7 +409,7 @@ def tile_list_mixing_closure_kernel(
         quantize_h(4, both)
         numerator(1)
         denominator(3)
-        denominator(4)
         numerator(2)
+        denominator(4)
         numerator(3)
         numerator(4)

@@ -66,11 +66,8 @@ def tile_list_mixing_closure_kernel(
         def staged(shape, dtype, name):
             return stage.tile(shape, dtype, name=name, offset=place[name], align_bytes=64)
 
-        pairs = [0, 1, 2, 3, 0, 1, 2, 1, 0, 2, 3, 1] + [0, 2, 3, 1] * 2 + [0]
-        bank_order = [2 * pair + x for pair in pairs for x in range(2)] + [4, 6, 7, 5, 2, 3, 0, 1]
-
-        def new_bank():
-            return psum.tile([P, BANK], F32, name=f"bank{bank_order.pop(0)}")
+        def new_bank(number):
+            return psum.tile([P, BANK], F32, name=f"bank{number}")
 
         offsets = lists.tile([P, S // 16], U16, name="offsets")
         nc.sync.dma_start(offsets[:], offs)
@@ -164,11 +161,11 @@ def tile_list_mixing_closure_kernel(
                 stop=stop,
             )
 
-        def strat_banks(half, b, slots, by_pass=False):
+        def strat_banks(half, b, slots, numbers, by_pass=False):
             for quarter in sorted({2 * half + slot // 2 for slot in slots}):
                 name = f"strat{b}_{quarter}"
                 strat[b, quarter] = (staged if name in place else held)([P, 2, WIDE, 2], F32, name)
-            banks = {slot: new_bank()[:].rearrange("p (e j) -> p e j", e=2) for slot in slots}
+            banks = {slot: new_bank(x)[:].rearrange("p (e j) -> p e j", e=2) for slot, x in zip(slots, numbers)}
             if by_pass:
                 for a in range(PASSES):
                     for slot in slots:
@@ -222,8 +219,8 @@ def tile_list_mixing_closure_kernel(
         deal_plane(1)
         deal_words(1)
         gather_words(1, 0)
-        strat_banks(0, 0, range(PACK), by_pass=True)
-        strat_banks(0, 1, range(PACK))
+        strat_banks(0, 0, range(PACK), range(4), by_pass=True)
+        strat_banks(0, 1, range(PACK), range(4, 8))
         gather_words(0, 1)
         gather_words(1, 1)
         low = [group_ws(a, 0, [nc.vector.tensor_copy]) for a in range(PASSES)]
@@ -236,28 +233,39 @@ def tile_list_mixing_closure_kernel(
         h_codes = [held([P, PASSES, widths[x]], U32, f"h_codes{x}") for x in range(pieces)]
         h_plane = [held([P, PASSES, widths[x]], U8, f"h_plane{x}") for x in range(pieces)]
 
-        def make_h(piece, b):
-            lo, hi = OUT_CUTS[piece], OUT_CUTS[piece + 1]
-            for jb in range(lo // JB, hi // JB):
-                bank = new_bank()[:].rearrange("p (t j) -> p t j", t=PACK)
-                half, first = divmod(jb * JB, BANK)
-                for t in range(PACK):
-                    for a in range(PASSES):
-                        nc.tensor.matmul_mx(
-                            out=bank[:, t, :],
-                            lhsT=ws_codes[a, b][:, t * P : (t + 1) * P].bitcast(FP8X4),
-                            lhsT_scale=ws_plane[a, b][:, t * P : (t + 1) * P],
-                            rhs=v_codes[a][half][:, first : first + JB].bitcast(FP8X4),
-                            rhs_scale=v_scales[:, a, jb * JB : (jb + 1) * JB],
-                            start=(a == 0),
-                            stop=(a == PASSES - 1),
-                        )
-                nc.vector.tensor_tensor(
-                    h[piece][:, b, jb * JB - lo : (jb + 1) * JB - lo, :].rearrange("p j (u e) -> p j u e", e=2),
-                    bank.rearrange("p (u e) j -> p j u e", e=2),
-                    strat[b, jb // 2][:, :, jb % 2 * JB : (jb % 2 + 1) * JB, :].rearrange("p u j e -> p j u e"),
-                    MULT,
+        shear = {}
+
+        def shear_sum(jb, b, number, by_pass=False):
+            bank = new_bank(number)[:].rearrange("p (t j) -> p t j", t=PACK)
+            half, first = divmod(jb * JB, BANK)
+            order = [(t, a, a == 0, a == PASSES - 1) for t in range(PACK) for a in range(PASSES)]
+            if by_pass:
+                order = [(t, a, a + t == 0, a + t == PASSES + PACK - 2) for a in range(PASSES) for t in range(PACK)]
+            for t, a, start, stop in order:
+                nc.tensor.matmul_mx(
+                    out=bank[:, t, :],
+                    lhsT=ws_codes[a, b][:, t * P : (t + 1) * P].bitcast(FP8X4),
+                    lhsT_scale=ws_plane[a, b][:, t * P : (t + 1) * P],
+                    rhs=v_codes[a][half][:, first : first + JB].bitcast(FP8X4),
+                    rhs_scale=v_scales[:, a, jb * JB : (jb + 1) * JB],
+                    start=start,
+                    stop=stop,
                 )
+            shear[jb, b] = bank
+
+        def product(jb, b):
+            piece = max(x for x in range(pieces) if OUT_CUTS[x] <= jb * JB)
+            lo = jb * JB - OUT_CUTS[piece]
+            nc.vector.tensor_tensor(
+                h[piece][:, b, lo : lo + JB, :].rearrange("p j (u e) -> p j u e", e=2),
+                shear[jb, b].rearrange("p (u e) j -> p j u e", e=2),
+                strat[b, jb // 2][:, :, jb % 2 * JB : (jb % 2 + 1) * JB, :].rearrange("p u j e -> p j u e"),
+                MULT,
+            )
+
+        def make_h(jb, b, number, by_pass=False):
+            shear_sum(jb, b, number, by_pass)
+            product(jb, b)
 
         def quantize_h(piece, blocks):
             nc.vector.quantize_mx(
@@ -305,13 +313,13 @@ def tile_list_mixing_closure_kernel(
                     in_=wn_grouped[:, PACK * lo : PACK * hi],
                 )
 
-        def second_stage(piece, codes, plane):
+        def second_stage(piece, codes, plane, numbers):
             width = widths[piece]
-            per_bank = 2 if piece == pieces - 1 else min(N_TILES, BANK // width)
+            per_bank = -(-N_TILES // len(numbers))
             banks = []
-            for first in range(0, N_TILES, per_bank):
+            for first, number in zip(range(0, N_TILES, per_bank), numbers):
                 rows = range(first, min(first + per_bank, N_TILES))
-                bank = new_bank()[:, : len(rows) * width].rearrange("p (c j) -> p c j", j=width)
+                bank = new_bank(number)[:, : len(rows) * width].rearrange("p (c j) -> p c j", j=width)
                 for c in rows:
                     for b in range(PASSES):
                         cols = slice(b * N + c * P, b * N + (c + 1) * P)
@@ -373,43 +381,49 @@ def tile_list_mixing_closure_kernel(
         recips = {}
         both = slice(0, PASSES)
 
-        def denominator(piece):
-            recips[piece] = reciprocal_of_denominator(second_stage(piece, wd_flat, wd_plane_flat), widths[piece])
+        def denominator(piece, numbers):
+            recips[piece] = reciprocal_of_denominator(second_stage(piece, wd_flat, wd_plane_flat, numbers), widths[piece])
 
-        def numerator(piece):
-            finish(piece, second_stage(piece, wn_codes, wn_plane), recips[piece])
+        def numerator(piece, numbers):
+            finish(piece, second_stage(piece, wn_codes, wn_plane, numbers), recips[piece])
 
         high = [group_ws(0, 1, [nc.scalar.copy])]
-        strat_banks(1, 0, (0, 1))
-        make_h(0, 0)
-        make_h(1, 0)
+        strat_banks(1, 0, (0, 1), (0, 1))
+        for jb in range(4):
+            make_h(jb, 0, 2 + jb, by_pass=jb < 2)
         high.append(group_ws(1, 1, [nc.vector.tensor_copy]))
         for a in range(PASSES):
             quantize_ws(a, 1, high[a])
+        quantize_h(0, slice(0, 1))
+        quantize_h(1, slice(0, 1))
         wn_grouped = group_wn()
-        strat_banks(1, 0, (2, 3))
-        strat_banks(1, 1, range(PACK))
-        make_h(0, 1)
-        quantize_h(0, both)
-        make_h(1, 1)
-        quantize_h(1, both)
-        make_h(2, 0)
-        denominator(0)
-        make_h(2, 1)
+        strat_banks(1, 0, (2, 3), (2, 3))
+        strat_banks(1, 1, range(PACK), (0, 1, 4, 5))
+        make_h(0, 1, 6, by_pass=True)
+        make_h(1, 1, 7, by_pass=True)
+        quantize_h(0, slice(1, 2))
+        make_h(2, 1, 2)
+        make_h(3, 1, 3)
+        quantize_h(1, slice(1, 2))
+        make_h(4, 0, 0)
+        make_h(5, 0, 1)
+        denominator(0, (4, 5))
+        make_h(4, 1, 6)
+        make_h(5, 1, 7)
         quantize_h(2, both)
-        denominator(1)
+        denominator(1, (2, 3))
         quantize_wn()
-        make_h(3, 0)
-        make_h(3, 1)
+        make_h(6, 0, 0)
+        make_h(6, 1, 1)
         quantize_h(3, both)
-        numerator(0)
-        denominator(2)
-        make_h(4, 0)
-        make_h(4, 1)
+        numerator(0, (4, 5))
+        denominator(2, (6, 7))
+        make_h(7, 0, 2)
+        make_h(7, 1, 3)
         quantize_h(4, both)
-        numerator(1)
-        denominator(3)
-        numerator(2)
-        denominator(4)
-        numerator(3)
-        numerator(4)
+        numerator(1, (0, 1))
+        denominator(3, (4,))
+        numerator(2, (6, 7))
+        denominator(4, (5, 2))
+        numerator(3, (3,))
+        numerator(4, (0, 1))

@@ -390,7 +390,7 @@ def tile_list_mixing_closure_kernel(
         high = [group_ws(0, 1, [nc.scalar.copy])]
         strat_banks(1, 0, (0, 1), (0, 1))
         for jb in range(4):
-            make_h(jb, 0, 2 + jb, by_pass=jb < 2)
+            make_h(jb, 0, 2 + jb, by_pass=jb < 1)
         high.append(group_ws(1, 1, [nc.vector.tensor_copy]))
         for a in range(PASSES):
             quantize_ws(a, 1, high[a])
@@ -400,7 +400,7 @@ def tile_list_mixing_closure_kernel(
         strat_banks(1, 0, (2, 3), (2, 3))
         strat_banks(1, 1, range(PACK), (0, 1, 4, 5))
         make_h(0, 1, 6, by_pass=True)
-        make_h(1, 1, 7, by_pass=True)
+        make_h(1, 1, 7)
         quantize_h(0, slice(1, 2))
         make_h(2, 1, 2)
         make_h(3, 1, 3)

@@ -355,7 +355,7 @@ def tile_list_mixing_closure_kernel(
             ratio = work.tile(shape, F32, name="ratio", bufs=3)
             result = held(shape, F32, f"result{piece}")
             rows_out = out.rearrange("(c p) j -> p c j", p=P)
-            if piece == pieces - 1:
+            if piece >= pieces - 2:
                 for rows, bank in num:
                     nc.vector.tensor_tensor(ratio[:, rows, :], bank, recip[:, rows, :], MULT)
                 for rows, bank in num:
@@ -370,9 +370,9 @@ def tile_list_mixing_closure_kernel(
             else:
                 for c in range(N_TILES):
                     nc.gpsimd.tensor_scalar(result[:, c, :], ratio[:, c, :], 1.0, kb_cols[:, c : c + 1], MULT, ADD)
-                    if hi == VECTOR_ADDS_FROM:
+                    if 0 < lo < VECTOR_ADDS_FROM:
                         nc.sync.dma_start(rows_out[:, c, lo:hi], result[:, c, :])
-                if hi == VECTOR_ADDS_FROM:
+                if 0 < lo < VECTOR_ADDS_FROM:
                     return
             nc.sync.dma_start(out.rearrange("(c p) j -> p c j", p=P)[:, :, lo:hi], result[:])
 
@@ -422,8 +422,8 @@ def tile_list_mixing_closure_kernel(
         make_h(7, 1, 3)
         quantize_h(4, both)
         numerator(1, (0, 1))
-        denominator(3, (4,))
+        denominator(3, (4, 5))
         numerator(2, (6, 7))
-        denominator(4, (5, 2))
-        numerator(3, (3,))
+        denominator(4, (2, 3))
+        numerator(3, (4,))
         numerator(4, (0, 1))

@@ -128,9 +128,9 @@ def tile_list_mixing_closure_kernel(
         def deal_words(a):
             for b in range(PASSES):
                 cols = slice(b * H, (b + 1) * H)
-                nc.gpsimd.tensor_copy(
-                    wb_codes[a][:, cols].rearrange("p (t m e) -> p t m e", t=PACK, e=2),
-                    wb_raw[a][:, cols].rearrange("p (m t e) -> p t m e", t=PACK, e=2),
+                nc.scalar.copy(
+                    wb_codes[a][:, cols].bitcast(U16).rearrange("p (t m) -> p t m", t=PACK),
+                    wb_raw[a][:, cols].bitcast(U16).rearrange("p (m t) -> p t m", t=PACK),
                 )
 
         def deal_plane(a):

@@ -25,7 +25,7 @@ JB = 128
 BANK = 512
 WIDE = 256
 LAP = 64
-WARM_PASSES = 3
+WARM_PASSES = 2
 VECTOR_ADDS_FROM = 768
 WN_STEP = 96
 N_TILES = N // P
@@ -50,7 +50,8 @@ def tile_list_mixing_closure_kernel(
         cursor = 0
         for chain in (
             (("wd_codes", 8 * N), ("ws_raw10", 4 * T), ("tab_scale_win", T), ("ws_raw00", 4 * T), ("wd_plane", 2 * N)),
-            (("ws_raw01", 4 * T), ("picked", S), ("ws_raw11", 4 * T), ("kb_cols", 2 * LAP)),
+            (("picked1", BANK), ("wb_raw0", 2 * H), ("wb_raw1", 2 * H), ("ws_raw01", 4 * T)),
+            (("wb_scale_raw", 2 * H), ("ws_raw11", 4 * T), ("kb_cols", 2 * LAP)),
             (("wn_raw0", 16 * N), ("tab_win1", 4 * T), ("wn_raw1", 16 * N)),
         ):
             for name, size in chain:
@@ -74,16 +75,17 @@ def tile_list_mixing_closure_kernel(
 
         tab_scale_win = staged([P, T], U8, "tab_scale_win")
         nc.gpsimd.memset(tab_scale_win[:].bitcast(I32), 0)
-        wb_scale_raw = held([P, PASSES, H], U8, "wb_scale_raw")
+        wb_scale_raw = staged([P, PASSES, H], U8, "wb_scale_raw")
         nc.gpsimd.memset(wb_scale_raw[:].bitcast(I32), 0)
-        v_scales = held([P, PASSES, S], U8, "v_scales")
-        nc.gpsimd.memset(v_scales[:].bitcast(I32), 0)
+        v_scales = [held([P, PASSES, BANK], U8, f"v_scales{half}") for half in range(2)]
+        for half in range(2):
+            nc.gpsimd.memset(v_scales[half][:].bitcast(I32), 0)
 
         warm = held([P, 1], F32, "warm")
         nc.vector.memset(warm[:], 1.0)
         nc.scalar.activation(warm[:], warm[:], ACT.Abs_reciprocal_sqrt)
 
-        wb_raw = [held([P, 2 * H], U8, "wb_raw0"), held([P, 2 * H], U8, "wb_raw1")]
+        wb_raw = [staged([P, 2 * H], U8, f"wb_raw{a}") for a in range(PASSES)]
         nc.sync.dma_start(
             tab_scale_win[0:P:4, :].bitcast(I32), tab_scales.rearrange("a q t -> q a t").bitcast(I32)
         )
@@ -107,21 +109,6 @@ def tile_list_mixing_closure_kernel(
             nc.sync.dma_start(
                 wb_scale_raw[c:P:32].bitcast(I32), wb_scales[:, c:16:4, :].rearrange("a d n -> d a n").bitcast(I32)
             )
-        nc.sync.dma_start(wb_raw[1][:].bitcast(I32), wb_words[1].bitcast(I32))
-        load_table(1)
-
-        picked = staged([P, S], U8, "picked")
-        nc.vector.tensor_copy(picked[:], tab_scale_win[:].indirect(offsets[:]))
-        for d in (0, 2, 1, 3):
-            nc.sync.dma_start(
-                v_scales[32 * d : 32 * d + 4].bitcast(I32), picked[32 * d : 32 * d + 32 : 4, :].bitcast(I32)
-            )
-
-        load_ws(0, 0)
-        load_ws(1, 0)
-        for a in range(PASSES):
-            load_ws(a, 1)
-
         wb_codes = [held([P, 2 * H], U8, f"wb_codes{a}") for a in range(PASSES)]
         wb_plane = [held([P, H], U8, f"wb_plane{a}") for a in range(PASSES)]
 
@@ -138,6 +125,33 @@ def tile_list_mixing_closure_kernel(
                 wb_plane[a][:].rearrange("p (b t m) -> p b t m", b=PASSES, t=PACK),
                 wb_scale_raw[:, a, :].rearrange("p (b m t) -> p b t m", b=PASSES, t=PACK),
             )
+
+        def gather_scales(half):
+            picked = (held, staged)[half]([P, BANK], U8, f"picked{half}")
+            cols = slice(half * BANK // 16, (half + 1) * BANK // 16)
+            nc.vector.tensor_copy(picked[:], tab_scale_win[:].indirect(offsets[:, cols]))
+            return picked
+
+        def move_scales(half, picked):
+            for d in (0, 2, 1, 3):
+                nc.sync.dma_start(
+                    v_scales[half][32 * d : 32 * d + 4].bitcast(I32), picked[32 * d : 32 * d + 32 : 4, :].bitcast(I32)
+                )
+
+        load_table(1)
+        deal_words(0)
+        picked = gather_scales(0)
+        move_scales(0, picked)
+        nc.sync.dma_start(wb_raw[1][:].bitcast(I32), wb_words[1].bitcast(I32))
+        picked_late = gather_scales(1)
+        load_ws(0, 0)
+        move_scales(1, picked_late)
+        load_ws(1, 0)
+        deal_words(1)
+        for a in range(PASSES):
+            deal_plane(a)
+        for a in range(PASSES):
+            load_ws(a, 1)
 
         v_codes = [[held([P, BANK], U32, f"v_codes{a}{half}") for half in range(2)] for a in range(PASSES)]
 
@@ -156,7 +170,7 @@ def tile_list_mixing_closure_kernel(
                 lhsT=wb_codes[a][:, 2 * col : 2 * (col + P)].bitcast(FP4X4),
                 lhsT_scale=wb_plane[a][:, col : col + P],
                 rhs=v_codes[a][half][:, first : first + WIDE].bitcast(FP8X4),
-                rhs_scale=v_scales[:, a, half * BANK + first : half * BANK + first + WIDE],
+                rhs_scale=v_scales[half][:, a, first : first + WIDE],
                 start=start,
                 stop=stop,
             )
@@ -202,9 +216,7 @@ def tile_list_mixing_closure_kernel(
                 in_=grouped[:].rearrange("p t m i -> p (t m i)"),
             )
 
-        deal_words(0)
         gather_words(0, 0)
-        deal_plane(0)
         idle_bank = psum.tile([P, BANK], F32, name="bank7")
         for x in range(WARM_PASSES):
             nc.tensor.matmul_mx(
@@ -216,8 +228,6 @@ def tile_list_mixing_closure_kernel(
                 start=True,
                 stop=True,
             )
-        deal_plane(1)
-        deal_words(1)
         gather_words(1, 0)
         strat_banks(0, 0, range(PACK), range(4), by_pass=True)
         strat_banks(0, 1, range(PACK), range(4, 8))
@@ -247,7 +257,7 @@ def tile_list_mixing_closure_kernel(
                     lhsT=ws_codes[a, b][:, t * P : (t + 1) * P].bitcast(FP8X4),
                     lhsT_scale=ws_plane[a, b][:, t * P : (t + 1) * P],
                     rhs=v_codes[a][half][:, first : first + JB].bitcast(FP8X4),
-                    rhs_scale=v_scales[:, a, jb * JB : (jb + 1) * JB],
+                    rhs_scale=v_scales[half][:, a, first : first + JB],
                     start=start,
                     stop=stop,
                 )

@@ -85,11 +85,16 @@ def tile_list_mixing_closure_kernel(
         nc.vector.memset(warm[:], 1.0)
         nc.scalar.activation(warm[:], warm[:], ACT.Abs_reciprocal_sqrt)
 
-        wb_raw = [staged([P, 2 * H], U8, f"wb_raw{a}") for a in range(PASSES)]
+        wb_raw = [staged([P, PASSES, H], U8, f"wb_raw{b}") for b in range(PASSES)]
+
+        def load_wb(b):
+            words = wb_words[:, :, b * H : (b + 1) * H].rearrange("a p n -> p a n")
+            nc.sync.dma_start(wb_raw[b][:].bitcast(I32), words.bitcast(I32))
+
         nc.sync.dma_start(
             tab_scale_win[0:P:4, :].bitcast(I32), tab_scales.rearrange("a q t -> q a t").bitcast(I32)
         )
-        nc.sync.dma_start(wb_raw[0][:].bitcast(I32), wb_words[0].bitcast(I32))
+        load_wb(0)
         tab_win = []
 
         def load_table(a):
@@ -112,18 +117,19 @@ def tile_list_mixing_closure_kernel(
         wb_codes = [held([P, 2 * H], U8, f"wb_codes{a}") for a in range(PASSES)]
         wb_plane = [held([P, H], U8, f"wb_plane{a}") for a in range(PASSES)]
 
-        def deal_words(a):
-            for b in range(PASSES):
+        def deal_words(b):
+            for a in range(PASSES):
                 cols = slice(b * H, (b + 1) * H)
                 nc.scalar.copy(
                     wb_codes[a][:, cols].bitcast(U16).rearrange("p (t m) -> p t m", t=PACK),
-                    wb_raw[a][:, cols].bitcast(U16).rearrange("p (m t) -> p t m", t=PACK),
+                    wb_raw[b][:, a, :].bitcast(U16).rearrange("p (m t) -> p t m", t=PACK),
                 )
 
-        def deal_plane(a):
+        def deal_plane(a, b):
+            cols = slice(b * K_PASS, (b + 1) * K_PASS)
             nc.gpsimd.tensor_copy(
-                wb_plane[a][:].rearrange("p (b t m) -> p b t m", b=PASSES, t=PACK),
-                wb_scale_raw[:, a, :].rearrange("p (b m t) -> p b t m", b=PASSES, t=PACK),
+                wb_plane[a][:, cols].rearrange("p (t m) -> p t m", t=PACK),
+                wb_scale_raw[:, a, cols].rearrange("p (m t) -> p t m", t=PACK),
             )
 
         def gather_scales(half):
@@ -142,14 +148,15 @@ def tile_list_mixing_closure_kernel(
         deal_words(0)
         picked = gather_scales(0)
         move_scales(0, picked)
-        nc.sync.dma_start(wb_raw[1][:].bitcast(I32), wb_words[1].bitcast(I32))
+        load_wb(1)
         picked_late = gather_scales(1)
         load_ws(0, 0)
         move_scales(1, picked_late)
         load_ws(1, 0)
         deal_words(1)
-        for a in range(PASSES):
-            deal_plane(a)
+        for b in range(PASSES):
+            for a in range(PASSES):
+                deal_plane(a, b)
         for a in range(PASSES):
             load_ws(a, 1)
 

@@ -25,7 +25,6 @@ JB = 128
 BANK = 512
 WIDE = 256
 LAP = 64
-WARM_PASSES = 2
 VECTOR_ADDS_FROM = 768
 WN_STEP = 96
 N_TILES = N // P
@@ -224,17 +223,6 @@ def tile_list_mixing_closure_kernel(
             )
 
         gather_words(0, 0)
-        idle_bank = psum.tile([P, BANK], F32, name="bank7")
-        for x in range(WARM_PASSES):
-            nc.tensor.matmul_mx(
-                out=idle_bank[:],
-                lhsT=wb_codes[0][:, : 2 * P].bitcast(FP4X4),
-                lhsT_scale=wb_plane[0][:, :P],
-                rhs=v_codes[0][0][:].bitcast(FP8X4),
-                rhs_scale=picked[:, :BANK],
-                start=True,
-                stop=True,
-            )
         gather_words(1, 0)
         strat_banks(0, 0, range(PACK), range(4), by_pass=True)
         strat_banks(0, 1, range(PACK), range(4, 8))

@@ -204,12 +204,12 @@ def tile_list_mixing_closure_kernel(
 
         def group_ws(a, b, copies):
             grouped = (staged if a + b == 2 else held)([P, PACK, P, PACK], BF16, f"ws_grouped{a}{b}")
-            count = P // len(copies)
+            count = 2 // len(copies)
             for part, copy in enumerate(copies):
-                ms = slice(part * count, (part + 1) * count)
+                us = slice(part * count, (part + 1) * count)
                 copy(
-                    grouped[:, :, ms, :].rearrange("p (u e) m i -> p m u i e", e=2),
-                    ws_raw[a, b][:].rearrange("p i (m u e) -> p m u i e", u=2, e=2)[:, ms],
+                    grouped[:].rearrange("p (u e) m i -> p m u i e", e=2)[:, :, us],
+                    ws_raw[a, b][:].rearrange("p i (m u e) -> p m u i e", u=2, e=2)[:, :, us],
                 )
             return grouped
 
@@ -396,7 +396,7 @@ def tile_list_mixing_closure_kernel(
         strat_banks(1, 0, (0, 1), (0, 1))
         for jb in range(4):
             make_h(jb, 0, 2 + jb, by_pass=jb < 1)
-        high.append(group_ws(1, 1, [nc.vector.tensor_copy]))
+        high.append(group_ws(1, 1, [nc.vector.tensor_copy, nc.scalar.copy]))
         for a in range(PASSES):
             quantize_ws(a, 1, high[a])
         quantize_h(0, slice(0, 1))

from contextlib import ExitStack

import concourse.mybir as mybir

K, T, S, H, N = 1024, 2048, 1024, 1024, 384
FLOPS = 2 * (2 * K * H * S + 2 * H * N * S)

F32 = mybir.dt.float32
BF16 = mybir.dt.bfloat16
I32 = mybir.dt.int32
U32 = mybir.dt.uint32
U16 = mybir.dt.uint16
U8 = mybir.dt.uint8
FP8X4 = mybir.dt.float8_e4m3fn_x4
FP4X4 = mybir.dt.float4_e2m1fn_x4
ACT = mybir.ActivationFunctionType
MULT = mybir.AluOpType.mult
ADD = mybir.AluOpType.add

P = 128
PACK = 4
K_PASS = P * PACK
PASSES = 2
JB = 128
BANK = 512
WIDE = 256
LAP = 64
VECTOR_ADDS_FROM = 768
WN_STEP = 96
N_TILES = N // P
OUT_CUTS = (0, 256, 512, 768, 896, 1024)


def tile_list_mixing_closure_kernel(
    tc, tab_words, tab_scales, offs, ws, wb_words, wb_scales, wn, wd_words, wd_scales, kb, out
):
    nc = tc.nc
    with ExitStack() as ctx:
        lists = ctx.enter_context(tc.tile_pool(name="lists", bufs=1))
        keep = ctx.enter_context(tc.tile_pool(name="keep", bufs=1))
        stage = ctx.enter_context(tc.tile_pool(name="stage", bufs=1))
        work = ctx.enter_context(tc.tile_pool(name="work", bufs=2))
        psum = ctx.enter_context(tc.psum_pool(name="psum", bufs=1))

        def held(shape, dtype, name):
            return keep.tile(shape, dtype, name=name, align_bytes=64)

        place = {}
        cursor = 0
        for chain in (
            (("wd_codes", 8 * N), ("ws_raw10", 4 * T), ("tab_scale_win", T), ("ws_raw00", 4 * T), ("wd_plane", 2 * N)),
            (("picked1", BANK), ("wb_raw0", 2 * H), ("wb_raw1", 2 * H), ("ws_raw01", 4 * T)),
            (("wb_scale_raw", 2 * H), ("ws_raw11", 4 * T), ("kb_cols", 2 * LAP)),
            (("wn_raw0", 16 * N), ("tab_win1", 4 * T), ("wn_raw1", 16 * N)),
        ):
            for name, size in chain:
                place[name] = cursor
                cursor += size - LAP
            cursor += LAP
        place["strat0_3"] = place["ws_raw01"] + 2 * T - LAP - LAP + 2 * LAP
        place["strat0_2"] = place["ws_raw01"]
        place["strat0_1"] = cursor
        place["ws_grouped11"] = cursor + 2 * T - LAP
        place["wn_grouped"] = place["ws_grouped11"] + 2 * T - LAP

        def staged(shape, dtype, name):
            return stage.tile(shape, dtype, name=name, offset=place[name], align_bytes=64)

        def new_bank(number):
            return psum.tile([P, BANK], F32, name=f"bank{number}")

        offsets = lists.tile([P, S // 16], U16, name="offsets")
        nc.sync.dma_start(offsets[:], offs)

        tab_scale_win = staged([P, T], U8, "tab_scale_win")
        nc.gpsimd.memset(tab_scale_win[:].bitcast(I32), 0)
        wb_scale_raw = staged([P, PASSES, H], U8, "wb_scale_raw")
        nc.gpsimd.memset(wb_scale_raw[:].bitcast(I32), 0)
        v_scales = [held([P, PASSES, BANK], U8, f"v_scales{half}") for half in range(2)]
        for half in range(2):
            nc.gpsimd.memset(v_scales[half][:].bitcast(I32), 0)

        warm = held([P, 1], F32, "warm")
        nc.vector.memset(warm[:], 1.0)
        nc.scalar.activation(warm[:], warm[:], ACT.Abs_reciprocal_sqrt)

        wb_raw = [staged([P, PASSES, H], U8, f"wb_raw{b}") for b in range(PASSES)]

        def load_wb(b):
            words = wb_words[:, :, b * H : (b + 1) * H].rearrange("a p n -> p a n")
            nc.sync.dma_start(wb_raw[b][:].bitcast(I32), words.bitcast(I32))

        nc.sync.dma_start(
            tab_scale_win[0:P:4, :].bitcast(I32), tab_scales.rearrange("a q t -> q a t").bitcast(I32)
        )
        load_wb(0)
        tab_win = []

        def load_table(a):
            win = (held, staged)[a]([P, T], U32, f"tab_win{a}")
            nc.sync.dma_start(win[:].bitcast(I32), tab_words[a].rearrange("p t i -> p (t i)").bitcast(I32))
            tab_win.append(win)

        ws_raw = {}

        def load_ws(a, b):
            ws_raw[a, b] = staged([P, PACK, K_PASS], F32, f"ws_raw{a}{b}")
            rows = ws[a * K_PASS : (a + 1) * K_PASS, b * K_PASS : (b + 1) * K_PASS]
            nc.sync.dma_start(ws_raw[a, b][:], rows.rearrange("(p i) r -> p i r", i=PACK))

        load_table(0)
        for c in range(4):
            nc.sync.dma_start(
                wb_scale_raw[c:P:32].bitcast(I32), wb_scales[:, c:16:4, :].rearrange("a d n -> d a n").bitcast(I32)
            )
        wb_codes = [held([P, 2 * H], U8, f"wb_codes{a}") for a in range(PASSES)]
        wb_plane = [held([P, H], U8, f"wb_plane{a}") for a in range(PASSES)]

        def deal_words(b):
            for a in range(PASSES):
                cols = slice(b * H, (b + 1) * H)
                nc.scalar.copy(
                    wb_codes[a][:, cols].bitcast(U16).rearrange("p (t m) -> p t m", t=PACK),
                    wb_raw[b][:, a, :].bitcast(U16).rearrange("p (m t) -> p t m", t=PACK),
                )

        def deal_plane(a, b):
            cols = slice(b * K_PASS, (b + 1) * K_PASS)
            nc.gpsimd.tensor_copy(
                wb_plane[a][:, cols].rearrange("p (t m) -> p t m", t=PACK),
                wb_scale_raw[:, a, cols].rearrange("p (m t) -> p t m", t=PACK),
            )

        def gather_scales(half):
            picked = (held, staged)[half]([P, BANK], U8, f"picked{half}")
            cols = slice(half * BANK // 16, (half + 1) * BANK // 16)
            nc.vector.tensor_copy(picked[:], tab_scale_win[:].indirect(offsets[:, cols]))
            return picked

        def move_scales(half, picked):
            for d in (0, 2, 1, 3):
                nc.sync.dma_start(
                    v_scales[half][32 * d : 32 * d + 4].bitcast(I32), picked[32 * d : 32 * d + 32 : 4, :].bitcast(I32)
                )

        load_table(1)
        deal_words(0)
        picked = gather_scales(0)
        move_scales(0, picked)
        load_wb(1)
        picked_late = gather_scales(1)
        load_ws(0, 0)
        move_scales(1, picked_late)
        load_ws(1, 0)
        deal_words(1)
        for b in range(PASSES):
            for a in range(PASSES):
                deal_plane(a, b)
        for a in range(PASSES):
            load_ws(a, 1)

        v_codes = [[held([P, BANK], U32, f"v_codes{a}{half}") for half in range(2)] for a in range(PASSES)]

        def gather_words(a, half):
            cols = slice(half * BANK // 16, (half + 1) * BANK // 16)
            nc.vector.tensor_copy(v_codes[a][half][:], tab_win[a][:].indirect(offsets[:, cols]))

        strat = {}

        def strat_pass(bank, half, b, slot, e, a, start, stop):
            quarter, u = divmod(slot, 2)
            col = (b * PACK + 2 * u + e) * P
            first = quarter * WIDE
            nc.tensor.matmul_mx(
                out=bank[:, e, :],
                lhsT=wb_codes[a][:, 2 * col : 2 * (col + P)].bitcast(FP4X4),
                lhsT_scale=wb_plane[a][:, col : col + P],
                rhs=v_codes[a][half][:, first : first + WIDE].bitcast(FP8X4),
                rhs_scale=v_scales[half][:, a, first : first + WIDE],
                start=start,
                stop=stop,
            )

        def strat_banks(half, b, slots, numbers, by_pass=False):
            for quarter in sorted({2 * half + slot // 2 for slot in slots}):
                name = f"strat{b}_{quarter}"
                strat[b, quarter] = (staged if name in place else held)([P, 2, WIDE, 2], F32, name)
            banks = {slot: new_bank(x)[:].rearrange("p (e j) -> p e j", e=2) for slot, x in zip(slots, numbers)}
            if by_pass:
                for a in range(PASSES):
                    for slot in slots:
                        for e in range(2):
                            strat_pass(banks[slot], half, b, slot, e, a, a + e == 0, a + e == 2)
            else:
                for slot in slots:
                    for e in range(2):
                        for a in range(PASSES):
                            strat_pass(banks[slot], half, b, slot, e, a, a == 0, a == PASSES - 1)
            for slot in slots:
                quarter, u = divmod(slot, 2)
                nc.scalar.copy(strat[b, 2 * half + quarter][:, u], banks[slot].rearrange("p e j -> p j e"))

        ws_codes, ws_plane = {}, {}

        def group_ws(a, b, copies):
            grouped = (staged if a + b == 2 else held)([P, PACK, P, PACK], BF16, f"ws_grouped{a}{b}")
            count = 2 // len(copies)
            for part, copy in enumerate(copies):
                us = slice(part * count, (part + 1) * count)
                copy(
                    grouped[:].rearrange("p (u e) m i -> p m u i e", e=2)[:, :, us],
                    ws_raw[a, b][:].rearrange("p i (m u e) -> p m u i e", u=2, e=2)[:, :, us],
                )
            return grouped

        def quantize_ws(a, b, grouped):
            ws_codes[a, b] = held([P, K_PASS], U32, f"ws_codes{a}{b}")
            ws_plane[a, b] = held([P, K_PASS], U8, f"ws_plane{a}{b}")
            nc.vector.quantize_mx(
                out=ws_codes[a, b][:].bitcast(FP8X4),
                scales=ws_plane[a, b][:],
                in_=grouped[:].rearrange("p t m i -> p (t m i)"),
            )

        gather_words(0, 0)
        gather_words(1, 0)
        strat_banks(0, 0, range(PACK), range(4), by_pass=True)
        strat_banks(0, 1, range(PACK), range(4, 8))
        gather_words(0, 1)
        gather_words(1, 1)
        low = [group_ws(a, 0, [nc.vector.tensor_copy]) for a in range(PASSES)]
        for a in range(PASSES):
            quantize_ws(a, 0, low[a])

        pieces = len(OUT_CUTS) - 1
        widths = [OUT_CUTS[x + 1] - OUT_CUTS[x] for x in range(pieces)]
        h = [held([P, PASSES, widths[x], PACK], BF16, f"h{x}") for x in range(pieces)]
        h_codes = [held([P, PASSES, widths[x]], U32, f"h_codes{x}") for x in range(pieces)]
        h_plane = [held([P, PASSES, widths[x]], U8, f"h_plane{x}") for x in range(pieces)]

        shear = {}

        def shear_sum(jb, b, number, by_pass=False):
            bank = new_bank(number)[:].rearrange("p (t j) -> p t j", t=PACK)
            half, first = divmod(jb * JB, BANK)
            order = [(t, a, a == 0, a == PASSES - 1) for t in range(PACK) for a in range(PASSES)]
            if by_pass:
                order = [(t, a, a + t == 0, a + t == PASSES + PACK - 2) for a in range(PASSES) for t in range(PACK)]
            for t, a, start, stop in order:
                nc.tensor.matmul_mx(
                    out=bank[:, t, :],
                    lhsT=ws_codes[a, b][:, t * P : (t + 1) * P].bitcast(FP8X4),
                    lhsT_scale=ws_plane[a, b][:, t * P : (t + 1) * P],
                    rhs=v_codes[a][half][:, first : first + JB].bitcast(FP8X4),
                    rhs_scale=v_scales[half][:, a, first : first + JB],
                    start=start,
                    stop=stop,
                )
            shear[jb, b] = bank

        def product(jb, b):
            piece = max(x for x in range(pieces) if OUT_CUTS[x] <= jb * JB)
            lo = jb * JB - OUT_CUTS[piece]
            nc.vector.tensor_tensor(
                h[piece][:, b, lo : lo + JB, :].rearrange("p j (u e) -> p j u e", e=2),
                shear[jb, b].rearrange("p (u e) j -> p j u e", e=2),
                strat[b, jb // 2][:, :, jb % 2 * JB : (jb % 2 + 1) * JB, :].rearrange("p u j e -> p j u e"),
                MULT,
            )

        def make_h(jb, b, number, by_pass=False):
            shear_sum(jb, b, number, by_pass)
            product(jb, b)

        def quantize_h(piece, blocks):
            nc.vector.quantize_mx(
                out=h_codes[piece][:, blocks, :].rearrange("p b j -> p (b j)").bitcast(FP8X4),
                scales=h_plane[piece][:, blocks, :].rearrange("p b j -> p (b j)"),
                in_=h[piece][:, blocks].rearrange("p b j t -> p (b j t)"),
            )


        wd_codes = staged([P, PASSES, N], U32, "wd_codes")
        nc.sync.dma_start(wd_codes[:].bitcast(I32), wd_words.rearrange("a p n i -> p a (n i)").bitcast(I32))
        wd_plane = staged([P, PASSES, N], U8, "wd_plane")
        nc.gpsimd.memset(wd_plane[:].bitcast(I32), 0)
        for c in range(4):
            nc.sync.dma_start(
                wd_plane[c:P:32].bitcast(I32), wd_scales[:, c:16:4, :].rearrange("a d n -> d a n").bitcast(I32)
            )

        kb_cols = staged([P, N_TILES], F32, "kb_cols")
        with nc.allow_non_contiguous_dma(reason="one value of kb for each partition"):
            nc.sync.dma_start(kb_cols[:], kb.rearrange("(c p) -> p c", p=P))
        wn_raw = []
        for b in range(PASSES):
            wn_raw.append(staged([P, PACK, N], F32, f"wn_raw{b}"))
            nc.sync.dma_start(wn_raw[b][:], wn[b * K_PASS : (b + 1) * K_PASS, :].rearrange("(p i) n -> p i n", i=PACK))

        def group_wn():
            grouped = staged([P, PASSES, N, PACK], BF16, "wn_grouped")
            for b in range(PASSES):
                for first in range(0, N, WN_STEP):
                    ns = slice(first, first + WN_STEP)
                    nc.gpsimd.tensor_scalar(
                        grouped[:, b, ns, :], wn_raw[b][:, :, ns].rearrange("p i n -> p n i"), 1.0, 0.0, MULT, ADD
                    )
            return grouped[:].rearrange("p b n i -> p (b n i)")

        wn_codes = held([P, PASSES * N], U32, "wn_codes")
        wn_plane = held([P, PASSES * N], U8, "wn_plane")

        def quantize_wn():
            for lo, hi in ((0, 512), (512, 768)):
                nc.vector.quantize_mx(
                    out=wn_codes[:, lo:hi].bitcast(FP8X4),
                    scales=wn_plane[:, lo:hi],
                    in_=wn_grouped[:, PACK * lo : PACK * hi],
                )

        def second_stage(piece, codes, plane, numbers):
            width = widths[piece]
            per_bank = -(-N_TILES // len(numbers))
            banks = []
            for first, number in zip(range(0, N_TILES, per_bank), numbers):
                rows = range(first, min(first + per_bank, N_TILES))
                bank = new_bank(number)[:, : len(rows) * width].rearrange("p (c j) -> p c j", j=width)
                for c in rows:
                    for b in range(PASSES):
                        cols = slice(b * N + c * P, b * N + (c + 1) * P)
                        nc.tensor.matmul_mx(
                            out=bank[:, c - first, :],
                            lhsT=codes[:, cols].bitcast(FP8X4),
                            lhsT_scale=plane[:, cols],
                            rhs=h_codes[piece][:, b, :].bitcast(FP8X4),
                            rhs_scale=h_plane[piece][:, b, :],
                            start=(b == 0),
                            stop=(b == PASSES - 1),
                        )
                banks.append((slice(rows.start, rows.stop), bank))
            return banks

        def reciprocal_of_denominator(den, width):
            shape = [P, N_TILES, width]
            den_sq = work.tile(shape, F32, name="den_sq")
            root = work.tile(shape, F32, name="root")
            recip = work.tile(shape, F32, name="recip", bufs=5)
            for rows, bank in den:
                nc.scalar.activation(den_sq[:, rows, :], bank, ACT.Square)
            halves = (slice(0, 2), slice(2, 3))
            for rows in halves:
                nc.scalar.activation(root[:, rows, :], den_sq[:, rows, :], ACT.Abs_reciprocal_sqrt, bias=1.0)
            for rows in halves:
                nc.scalar.activation(recip[:, rows, :], root[:, rows, :], ACT.Square)
            return recip

        def finish(piece, num, recip):
            lo, hi = OUT_CUTS[piece], OUT_CUTS[piece + 1]
            shape = [P, N_TILES, hi - lo]
            ratio = work.tile(shape, F32, name="ratio", bufs=3)
            result = held(shape, F32, f"result{piece}")
            rows_out = out.rearrange("(c p) j -> p c j", p=P)
            if piece >= pieces - 2:
                for rows, bank in num:
                    nc.vector.tensor_tensor(ratio[:, rows, :], bank, recip[:, rows, :], MULT)
                for rows, bank in num:
                    for c in range(rows.start, rows.stop):
                        nc.vector.tensor_scalar(result[:, c, :], ratio[:, c, :], kb_cols[:, c : c + 1], None, ADD)
                    nc.sync.dma_start(rows_out[:, rows, lo:hi], result[:, rows, :])
                return
            for rows, bank in num:
                nc.vector.tensor_tensor(ratio[:, rows, :], bank, recip[:, rows, :], MULT)
            if lo >= VECTOR_ADDS_FROM:
                nc.vector.tensor_tensor(result[:], ratio[:], kb_cols[:].unsqueeze(2).to_broadcast(shape), ADD)
            else:
                for c in range(N_TILES):
                    nc.gpsimd.tensor_scalar(result[:, c, :], ratio[:, c, :], 1.0, kb_cols[:, c : c + 1], MULT, ADD)
                    if 0 < lo < VECTOR_ADDS_FROM:
                        nc.sync.dma_start(rows_out[:, c, lo:hi], result[:, c, :])
                if 0 < lo < VECTOR_ADDS_FROM:
                    return
            nc.sync.dma_start(out.rearrange("(c p) j -> p c j", p=P)[:, :, lo:hi], result[:])

        wd_flat = wd_codes[:].rearrange("p b n -> p (b n)")
        wd_plane_flat = wd_plane[:].rearrange("p b n -> p (b n)")
        recips = {}
        both = slice(0, PASSES)

        def denominator(piece, numbers):
            recips[piece] = reciprocal_of_denominator(second_stage(piece, wd_flat, wd_plane_flat, numbers), widths[piece])

        def numerator(piece, numbers):
            finish(piece, second_stage(piece, wn_codes, wn_plane, numbers), recips[piece])

        high = [group_ws(0, 1, [nc.scalar.copy])]
        strat_banks(1, 0, (0, 1), (0, 1))
        for jb in range(4):
            make_h(jb, 0, 2 + jb, by_pass=jb < 1)
        high.append(group_ws(1, 1, [nc.vector.tensor_copy, nc.scalar.copy]))
        for a in range(PASSES):
            quantize_ws(a, 1, high[a])
        quantize_h(0, slice(0, 1))
        quantize_h(1, slice(0, 1))
        wn_grouped = group_wn()
        strat_banks(1, 0, (2, 3), (2, 3))
        strat_banks(1, 1, range(PACK), (0, 1, 4, 5))
        make_h(0, 1, 6, by_pass=True)
        make_h(1, 1, 7)
        quantize_h(0, slice(1, 2))
        make_h(2, 1, 2)
        make_h(3, 1, 3)
        quantize_h(1, slice(1, 2))
        make_h(4, 0, 0)
        make_h(5, 0, 1)
        denominator(0, (4, 5))
        make_h(4, 1, 6)
        make_h(5, 1, 7)
        quantize_h(2, both)
        denominator(1, (2, 3))
        quantize_wn()
        make_h(6, 0, 0)
        make_h(6, 1, 1)
        quantize_h(3, both)
        numerator(0, (4, 5))
        denominator(2, (6, 7))
        make_h(7, 0, 2)
        make_h(7, 1, 3)
        quantize_h(4, both)
        numerator(1, (0, 1))
        denominator(3, (4, 5))
        numerator(2, (6, 7))
        denominator(4, (2, 3))
        numerator(3, (4,))
        numerator(4, (0, 1))
